import numpy as np
import ml_dtypes


def mxq(x, axis, fmt="e4m3"):
    dtype, down = {"e4m3": (ml_dtypes.float8_e4m3fn, 7), "e5m2": (ml_dtypes.float8_e5m2, 14)}[fmt]
    v = np.moveaxis(np.asarray(x, np.float32).astype(ml_dtypes.bfloat16).astype(np.float64), axis, -1)
    blocks = v.reshape(v.shape[:-1] + (-1, 32))
    amax = np.abs(blocks).max(-1, keepdims=True)
    byte = np.maximum(np.where(amax > 0, np.frexp(amax)[1] - 1 + 127, 0) - down, 1)
    scale = np.exp2(byte - 127.0)
    codes = (blocks / scale).astype(np.float32).astype(dtype).astype(np.float64)
    return np.moveaxis((codes * scale).reshape(v.shape), -1, axis)


WIDE = False


def mx_kscale(k):
    if not WIDE:
        return np.ones(k)
    levels = np.array([10, -10, 5, -5, 0])
    if k % 512:
        return np.exp2(np.random.permutation(np.resize(levels, k // 32))).repeat(32)
    a = np.empty((k // 512, 16))
    for p in range(k // 512):
        a[p, :8] = np.random.permutation(np.resize(levels, 8))
        for g in range(8):
            far = levels[np.abs(levels - a[p, g]) >= 10]
            a[p, g + 8] = far[np.random.randint(len(far))]
    return np.exp2(a.ravel()).repeat(32)


def f64(x):
    return np.asarray(x).astype(np.float64)


def striped(idx):
    return np.tile(idx.reshape(-1, 16).T, (8, 1)).astype(np.uint16)


def unstriped(offs):
    return offs[:16].T.reshape(-1).astype(np.int64)


def pack_weight(w):
    k, n = w.shape
    w = f64(np.asarray(w, np.float32).astype(ml_dtypes.bfloat16)).reshape(k // 32, 32, n)
    amax = np.abs(w).max(1)
    byte = np.clip(np.where(amax > 0, np.frexp(amax)[1] - 1 + 127 - 7, 1), 1, 254)
    scaled = (w * np.exp2(127.0 - byte)[:, None, :]).reshape(k, n).astype(np.float32)
    words = np.ascontiguousarray(scaled.reshape(k // 512, 128, 4, n).transpose(0, 1, 3, 2)).astype(ml_dtypes.float8_e4m3fn).view(np.uint8)
    return words, np.ascontiguousarray(byte.astype(np.uint8).reshape(k // 512, 16, n))


def unpack_weight(words, scales):
    g, p, n, _ = words.shape
    vals = np.ascontiguousarray(words).view(ml_dtypes.float8_e4m3fn).astype(np.float64) * np.repeat(np.exp2(scales.astype(np.float64) - 127.0), 8, axis=1)[..., None]
    return vals.transpose(0, 1, 3, 2).reshape(g * 512, n)

def planes(y):
    n, m = y.shape
    v = y.astype(np.float32).astype(ml_dtypes.bfloat16).astype(np.float64).reshape(n // 32, 32, m)
    top = np.abs(v).max(1)
    byte = np.clip(np.where(top > 0, np.frexp(top)[1] - 1 + 127 - 7, 1), 1, 254)
    codes = (v * np.exp2(127.0 - byte)[:, None, :]).reshape(n, m).astype(np.float32).astype(ml_dtypes.float8_e4m3fn).view(np.uint8)
    words = codes.reshape(n // 512, 128, 4, m).transpose(0, 1, 3, 2)
    return np.ascontiguousarray(words), np.ascontiguousarray(byte.astype(np.uint8).reshape(n // 512, 16, m))


K, T, S, H = 512, 1024, 512, 512


def setup_inputs():
    n = np.random.standard_normal
    s = mx_kscale(K)[:, None]
    u = mx_kscale(H)
    packed_xT = pack_weight(n((K, T)) * s)
    return {
        "x_words": packed_xT[0],
        "x_scales": packed_xT[1],
        "w1": (n((K, H)) / np.sqrt(K) / s * u).astype(np.float32),
        "w2": (n((H, H)) / np.sqrt(H) / u[:, None]).astype(np.float32),
        "pe": (0.5 * n((H, T)) * u[:, None]).astype(np.float32),
        "offs": striped(np.random.permutation(T)[:S]),
    }


def reference(x_words, x_scales, w1, w2, pe, offs):
    xq = unpack_weight(x_words, x_scales)[:, unstriped(offs)]
    g = f64(pe)[:, unstriped(offs)]
    h = (mxq(f64(w1), 0, "e4m3").T @ xq) + g
    out_0 = mxq(f64(w2), 0, "e4m3").T @ mxq(h, 0, "e4m3")
    return (out_0,) + planes(out_0)

@@ -1,0 +1,180 @@
+from contextlib import ExitStack
+
+import concourse.mybir as mybir
+
+K, T, S, H = 512, 1024, 512, 512
+FLOPS = 2 * K * H * S + 2 * H * H * S
+
+F32 = mybir.dt.float32
+BF16 = mybir.dt.bfloat16
+I32 = mybir.dt.int32
+U32 = mybir.dt.uint32
+U16 = mybir.dt.uint16
+U8 = mybir.dt.uint8
+FP8X4 = mybir.dt.float8_e4m3fn_x4
+ADD = mybir.AluOpType.add
+
+P = 128
+PACK = 4
+CH = 128
+NCH = S // CH
+
+
+def deal(engine_copy, grouped, raw, m0, m1, raw_m0):
+    engine_copy(
+        out=grouped[:, :, m0:m1, :].rearrange("p t m j -> p m j t"),
+        in_=raw[:, :, PACK * (m0 - raw_m0) : PACK * (m1 - raw_m0)].rearrange("p j (m t) -> p m j t", t=PACK),
+    )
+
+
+def woven(tile):
+    return tile.rearrange("p (c i) t -> p c t i", i=4)
+
+
+def planar(tile):
+    return tile.rearrange("p t (c i) -> p c t i", i=4)
+
+
+def tile_picked_posadd_none_po_kernel(
+    tc, x_words, x_scales, w1, w2, pe, offs, out_0, out_1, out_2
+):
+    nc = tc.nc
+    with ExitStack() as ctx:
+        keep = ctx.enter_context(tc.tile_pool(name="keep", bufs=1))
+        psum = ctx.enter_context(tc.psum_pool(name="psum", bufs=1))
+
+        offsets = keep.tile([P, S // 16], U16, name="offsets")
+        nc.sync.dma_start(offsets[:], offs)
+
+        xs_all = keep.tile([P, T], U8, name="xs_all", align_bytes=64)
+        nc.vector.memset(xs_all[:].bitcast(I32), 0)
+        pe_rows = pe.rearrange("(p t) c -> p t c", t=PACK)
+        pe_all = [keep.tile([P, T], F32, name=f"pe_all{t}") for t in range(PACK)]
+        nc.sync.dma_start(pe_all[0][:, : T // 2], pe_rows[:, 0, : T // 2])
+        for q in range(4):
+            nc.sync.dma_start(
+                xs_all[32 * q : 32 * q + 4, :].bitcast(I32), x_scales[0, 4 * q : 4 * q + 4, :].bitcast(I32)
+            )
+        nc.sync.dma_start(pe_all[0][:, T // 2 :], pe_rows[:, 0, T // 2 :])
+
+        w1_rows = w1.rearrange("(p j) c -> p j c", j=PACK)
+        w1_raw = [keep.tile([P, PACK, H // 2], F32, name=f"w1_raw{u}") for u in range(2)]
+        nc.sync.dma_start(w1_raw[0][:], w1_rows[:, :, : H // 2])
+        nc.sync.dma_start(pe_all[1][:], pe_rows[:, 1, :])
+        nc.sync.dma_start(w1_raw[1][:], w1_rows[:, :, H // 2 :])
+        for t in range(2, PACK):
+            nc.sync.dma_start(pe_all[t][:], pe_rows[:, t, :])
+        xw_all = keep.tile([P, T], U32, name="xw_all", align_bytes=64)
+        nc.sync.dma_start(xw_all[:].bitcast(I32), x_words[0].rearrange("p n t -> p (n t)").bitcast(I32))
+        w2_rows = w2.rearrange("(p j) c -> p j c", j=PACK)
+        w2_raw = [keep.tile([P, PACK, H // 2], F32, name=f"w2_raw{u}") for u in range(2)]
+        for u in range(2):
+            nc.sync.dma_start(w2_raw[u][:], w2_rows[:, :, u * (H // 2) : (u + 1) * (H // 2)])
+
+        g = keep.tile([P, PACK, S], F32, name="g")
+        xs = keep.tile([P, S], U8, name="xs", align_bytes=64)
+        nc.vector.tensor_copy(xs[:], xs_all[:].indirect(offsets[:]))
+
+        def weight_tiles(name):
+            bf = [keep.tile([P, PACK, P // 2, PACK], BF16, name=f"{name}_bf{u}", align_bytes=64) for u in range(2)]
+            words = keep.tile([P, H], U32, name=f"{name}_words", align_bytes=64)
+            scales = keep.tile([P, H], U8, name=f"{name}_scales", align_bytes=64)
+            return bf, words, scales
+
+        def quantize_weight_half(bf, words, scales, u):
+            for t in range(PACK):
+                cols = slice(t * P + u * P // 2, t * P + (u + 1) * P // 2)
+                nc.vector.quantize_mx(
+                    out=words[:, cols].bitcast(FP8X4), scales=scales[:, cols], in_=bf[u][:, t].rearrange("p m j -> p (m j)")
+                )
+
+        def gather_pe(t):
+            nc.vector.tensor_copy(g[:, t, :], pe_all[t][:].indirect(offsets[:]))
+
+        w1_bf, w1_words, w1_scales = weight_tiles("w1")
+        for u in range(2):
+            deal(nc.scalar.copy, w1_bf[u], w1_raw[u], 0, P // 2, 0)
+        gather_pe(0)
+        gather_pe(1)
+        quantize_weight_half(w1_bf, w1_words, w1_scales, 0)
+        gather_pe(2)
+        quantize_weight_half(w1_bf, w1_words, w1_scales, 1)
+        gather_pe(3)
+
+        def product(bank, w_words, w_scales, words, scales):
+            for t in range(PACK):
+                nc.tensor.matmul_mx(
+                    out=bank[:, t, :],
+                    lhsT=w_words[:, t * P : (t + 1) * P].bitcast(FP8X4),
+                    lhsT_scale=w_scales[:, t * P : (t + 1) * P],
+                    rhs=words.bitcast(FP8X4),
+                    rhs_scale=scales,
+                    start=True,
+                    stop=True,
+                )
+
+        xw = [keep.tile([P, CH], U32, name=f"xw{c}", align_bytes=64) for c in range(NCH)]
+        first = [psum.tile([P, PACK, CH], F32, name=f"first{c}") for c in range(NCH)]
+        for c in range(NCH):
+            nc.vector.tensor_copy(xw[c][:], xw_all[:].indirect(offsets[:, c * CH // 16 : (c + 1) * CH // 16]))
+            product(first[c], w1_words, w1_scales, xw[c][:], xs[:, c * CH : (c + 1) * CH])
+
+        w2_bf, w2_words, w2_scales = weight_tiles("w2")
+        for u in range(2):
+            deal(nc.scalar.copy, w2_bf[u], w2_raw[u], 0, P // 2, 0)
+
+        h_bf = [keep.tile([P, CH, PACK], BF16, name=f"h_bf{c}", align_bytes=64) for c in range(NCH)]
+        h_words = [keep.tile([P, CH], U32, name=f"h_words{c}", align_bytes=64) for c in range(NCH)]
+        h_scales = [keep.tile([P, CH], U8, name=f"h_scales{c}", align_bytes=64) for c in range(NCH)]
+
+        def add(c):
+            nc.vector.tensor_tensor(
+                woven(h_bf[c][:]), planar(first[c][:]), planar(g[:, :, c * CH : (c + 1) * CH]), ADD
+            )
+
+        def quantize_h(c):
+            nc.vector.quantize_mx(
+                out=h_words[c][:].bitcast(FP8X4), scales=h_scales[c][:], in_=h_bf[c][:].rearrange("p n t -> p (n t)")
+            )
+
+        add(0)
+        quantize_weight_half(w2_bf, w2_words, w2_scales, 0)
+        add(1)
+        quantize_h(0)
+        quantize_weight_half(w2_bf, w2_words, w2_scales, 1)
+        quantize_h(1)
+        add(2)
+        add(3)
+        quantize_h(2)
+        quantize_h(3)
+
+        second = [psum.tile([P, PACK, CH], F32, name=f"second{c}") for c in range(NCH)]
+        y = [keep.tile([P, PACK, CH], F32, name=f"y{c}") for c in range(NCH)]
+        y_bf = [keep.tile([P, CH, PACK], BF16, name=f"y_bf{c}", align_bytes=64) for c in range(NCH)]
+        y_words = keep.tile([P, S], U32, name="y_words", align_bytes=64)
+        y_scales = keep.tile([P, S], U8, name="y_scales", align_bytes=64)
+        out_rows = out_0.rearrange("(p t) n -> p t n", t=PACK)
+        out_words = out_1[0].rearrange("p n t -> p (n t)").bitcast(I32)
+
+        def quantize_y(c):
+            cols = slice(c * CH, (c + 1) * CH)
+            nc.vector.quantize_mx(
+                out=y_words[:, cols].bitcast(FP8X4), scales=y_scales[:, cols], in_=y_bf[c][:].rearrange("p n t -> p (n t)")
+            )
+
+        for c in range(NCH):
+            product(second[c], w2_words, w2_scales, h_words[c][:], h_scales[c][:])
+            nc.scalar.copy(out=y[c][:], in_=second[c][:])
+            nc.sync.dma_start(out_rows[:, :, c * CH : (c + 1) * CH], y[c][:])
+            nc.vector.tensor_copy(woven(y_bf[c][:]), planar(y[c][:]))
+            if c > 0:
+                quantize_y(c - 1)
+        last = (NCH - 1) * CH
+        nc.sync.dma_start(out_words[:, :last], y_words[:, :last].bitcast(I32))
+        quantize_y(NCH - 1)
+        nc.sync.dma_start(out_words[:, last:], y_words[:, last:].bitcast(I32))
+        for q in range(4):
+            queue = nc.scalar if q % 2 else nc.sync
+            queue.dma_start(
+                out_2[0, 4 * q : 4 * q + 4, :].bitcast(I32), y_scales[32 * q : 32 * q + 4, :].bitcast(I32)
+            )

@@ -22,8 +22,8 @@ NCH = S // CH
 
 def deal(engine_copy, grouped, raw, m0, m1, raw_m0):
     engine_copy(
-        out=grouped[:, :, m0:m1, :].rearrange("p t m j -> p m j t"),
-        in_=raw[:, :, PACK * (m0 - raw_m0) : PACK * (m1 - raw_m0)].rearrange("p j (m t) -> p m j t", t=PACK),
+        out=grouped[:, :, m0:m1, :].rearrange("p (u e) m j -> p u m j e", e=2),
+        in_=raw[:, :, PACK * (m0 - raw_m0) : PACK * (m1 - raw_m0)].rearrange("p j (m u e) -> p u m j e", u=2, e=2),
     )
 
 
@@ -59,13 +59,13 @@ def tile_picked_posadd_none_po_kernel(
 
         w1_rows = w1.rearrange("(p j) c -> p j c", j=PACK)
         w1_raw = [keep.tile([P, PACK, H // 2], F32, name=f"w1_raw{u}") for u in range(2)]
-        nc.sync.dma_start(w1_raw[0][:], w1_rows[:, :, : H // 2])
-        nc.sync.dma_start(pe_all[1][:], pe_rows[:, 1, :])
-        nc.sync.dma_start(w1_raw[1][:], w1_rows[:, :, H // 2 :])
-        for t in range(2, PACK):
+        for t in range(1, PACK - 1):
             nc.sync.dma_start(pe_all[t][:], pe_rows[:, t, :])
+        for u in range(2):
+            nc.sync.dma_start(w1_raw[u][:], w1_rows[:, :, u * (H // 2) : (u + 1) * (H // 2)])
         xw_all = keep.tile([P, T], U32, name="xw_all", align_bytes=64)
         nc.sync.dma_start(xw_all[:].bitcast(I32), x_words[0].rearrange("p n t -> p (n t)").bitcast(I32))
+        nc.sync.dma_start(pe_all[PACK - 1][:], pe_rows[:, PACK - 1, :])
         w2_rows = w2.rearrange("(p j) c -> p j c", j=PACK)
         w2_raw = [keep.tile([P, PACK, H // 2], F32, name=f"w2_raw{u}") for u in range(2)]
         for u in range(2):
@@ -75,31 +75,19 @@ def tile_picked_posadd_none_po_kernel(
         xs = keep.tile([P, S], U8, name="xs", align_bytes=64)
         nc.vector.tensor_copy(xs[:], xs_all[:].indirect(offsets[:]))
 
-        def weight_tiles(name):
-            bf = [keep.tile([P, PACK, P // 2, PACK], BF16, name=f"{name}_bf{u}", align_bytes=64) for u in range(2)]
-            words = keep.tile([P, H], U32, name=f"{name}_words", align_bytes=64)
-            scales = keep.tile([P, H], U8, name=f"{name}_scales", align_bytes=64)
-            return bf, words, scales
-
-        def quantize_weight_half(bf, words, scales, u):
-            for t in range(PACK):
-                cols = slice(t * P + u * P // 2, t * P + (u + 1) * P // 2)
-                nc.vector.quantize_mx(
-                    out=words[:, cols].bitcast(FP8X4), scales=scales[:, cols], in_=bf[u][:, t].rearrange("p m j -> p (m j)")
-                )
-
         def gather_pe(t):
             nc.vector.tensor_copy(g[:, t, :], pe_all[t][:].indirect(offsets[:]))
 
-        w1_bf, w1_words, w1_scales = weight_tiles("w1")
-        for u in range(2):
-            deal(nc.scalar.copy, w1_bf[u], w1_raw[u], 0, P // 2, 0)
-        gather_pe(0)
-        gather_pe(1)
-        quantize_weight_half(w1_bf, w1_words, w1_scales, 0)
-        gather_pe(2)
-        quantize_weight_half(w1_bf, w1_words, w1_scales, 1)
-        gather_pe(3)
+        w1_bf = keep.tile([P, PACK, P, PACK], BF16, name="w1_bf", align_bytes=64)
+        w1_words = keep.tile([P, H], U32, name="w1_words", align_bytes=64)
+        w1_scales = keep.tile([P, H], U8, name="w1_scales", align_bytes=64)
+        for t in range(PACK - 1):
+            gather_pe(t)
+        deal(nc.scalar.copy, w1_bf, w1_raw[0], 0, P // 2, 0)
+        deal(nc.vector.tensor_copy, w1_bf, w1_raw[1], P // 2, P, P // 2)
+        nc.vector.quantize_mx(
+            out=w1_words[:].bitcast(FP8X4), scales=w1_scales[:], in_=w1_bf[:].rearrange("p t m j -> p (t m j)")
+        )
 
         def product(bank, w_words, w_scales, words, scales):
             for t in range(PACK):
@@ -113,48 +101,61 @@ def tile_picked_posadd_none_po_kernel(
                     stop=True,
                 )
 
-        xw = [keep.tile([P, CH], U32, name=f"xw{c}", align_bytes=64) for c in range(NCH)]
+        xw_picked = keep.tile([P, S], U32, name="xw_picked", align_bytes=64)
+        xw = [xw_picked[:, c * CH : (c + 1) * CH] for c in range(NCH)]
         first = [psum.tile([P, PACK, CH], F32, name=f"first{c}") for c in range(NCH)]
+        nc.vector.tensor_copy(xw_picked[:], xw_all[:].indirect(offsets[:]))
+        gather_pe(PACK - 1)
         for c in range(NCH):
-            nc.vector.tensor_copy(xw[c][:], xw_all[:].indirect(offsets[:, c * CH // 16 : (c + 1) * CH // 16]))
-            product(first[c], w1_words, w1_scales, xw[c][:], xs[:, c * CH : (c + 1) * CH])
+            product(first[c], w1_words, w1_scales, xw[c], xs[:, c * CH : (c + 1) * CH])
 
-        w2_bf, w2_words, w2_scales = weight_tiles("w2")
+        w2_bf = keep.tile([P, PACK, P, PACK], BF16, name="w2_bf", align_bytes=64)
+        w2_words = keep.tile([P, H], U32, name="w2_words", align_bytes=64)
+        w2_scales = keep.tile([P, H], U8, name="w2_scales", align_bytes=64)
         for u in range(2):
-            deal(nc.scalar.copy, w2_bf[u], w2_raw[u], 0, P // 2, 0)
+            deal(nc.scalar.copy, w2_bf, w2_raw[u], u * P // 2, (u + 1) * P // 2, u * P // 2)
 
-        h_bf = [keep.tile([P, CH, PACK], BF16, name=f"h_bf{c}", align_bytes=64) for c in range(NCH)]
+        def quantize_w2(u):
+            cols = slice(2 * u * P, 2 * (u + 1) * P)
+            nc.vector.quantize_mx(
+                out=w2_words[:, cols].bitcast(FP8X4),
+                scales=w2_scales[:, cols],
+                in_=w2_bf[:, 2 * u : 2 * u + 2].rearrange("p t m j -> p (t m j)"),
+            )
+
+        h_own = [keep.tile([P, CH, PACK], BF16, name=f"h_bf{c}", align_bytes=64) for c in range(NCH - 1)]
+        h_bf = [tile[:] for tile in h_own] + [w2_bf[:, PACK - 1]]
         h_words = [keep.tile([P, CH], U32, name=f"h_words{c}", align_bytes=64) for c in range(NCH)]
         h_scales = [keep.tile([P, CH], U8, name=f"h_scales{c}", align_bytes=64) for c in range(NCH)]
 
         def add(c):
             nc.vector.tensor_tensor(
-                woven(h_bf[c][:]), planar(first[c][:]), planar(g[:, :, c * CH : (c + 1) * CH]), ADD
+                woven(h_bf[c]), planar(first[c][:]), planar(g[:, :, c * CH : (c + 1) * CH]), ADD
             )
 
         def quantize_h(c):
             nc.vector.quantize_mx(
-                out=h_words[c][:].bitcast(FP8X4), scales=h_scales[c][:], in_=h_bf[c][:].rearrange("p n t -> p (n t)")
+                out=h_words[c][:].bitcast(FP8X4), scales=h_scales[c][:], in_=h_bf[c].rearrange("p n t -> p (n t)")
             )
 
-        add(0)
-        quantize_weight_half(w2_bf, w2_words, w2_scales, 0)
-        add(1)
-        quantize_h(0)
-        quantize_weight_half(w2_bf, w2_words, w2_scales, 1)
-        quantize_h(1)
-        add(2)
-        add(3)
-        quantize_h(2)
-        quantize_h(3)
-
         second = [psum.tile([P, PACK, CH], F32, name=f"second{c}") for c in range(NCH)]
-        y = [keep.tile([P, PACK, CH], F32, name=f"y{c}") for c in range(NCH)]
+        y_tiles = [keep.tile([P, PACK, CH], F32, name=f"y{c}") for c in range(NCH)]
+        y = [tile[:] for tile in y_tiles]
         y_bf = [keep.tile([P, CH, PACK], BF16, name=f"y_bf{c}", align_bytes=64) for c in range(NCH)]
         y_words = keep.tile([P, S], U32, name="y_words", align_bytes=64)
         y_scales = keep.tile([P, S], U8, name="y_scales", align_bytes=64)
         out_rows = out_0.rearrange("(p t) n -> p t n", t=PACK)
         out_words = out_1[0].rearrange("p n t -> p (n t)").bitcast(I32)
+
+        def second_product(c):
+            product(second[c], w2_words, w2_scales, h_words[c][:], h_scales[c][:])
+
+        def copy_y(c):
+            nc.scalar.copy(out=y[c], in_=second[c][:])
+            nc.sync.dma_start(out_rows[:, :, c * CH : (c + 1) * CH], y[c])
+
+        def round_y(c, source):
+            nc.vector.tensor_copy(out=woven(y_bf[c][:]), in_=planar(source))
 
         def quantize_y(c):
             cols = slice(c * CH, (c + 1) * CH)
@@ -162,17 +163,32 @@ def tile_picked_posadd_none_po_kernel(
                 out=y_words[:, cols].bitcast(FP8X4), scales=y_scales[:, cols], in_=y_bf[c][:].rearrange("p n t -> p (n t)")
             )
 
+        add(0)
+        add(1)
+        quantize_h(0)
+        add(2)
+        quantize_h(1)
+        quantize_w2(0)
+        quantize_w2(1)
+        add(3)
+        quantize_h(2)
+        quantize_h(3)
         for c in range(NCH):
-            product(second[c], w2_words, w2_scales, h_words[c][:], h_scales[c][:])
-            nc.scalar.copy(out=y[c][:], in_=second[c][:])
-            nc.sync.dma_start(out_rows[:, :, c * CH : (c + 1) * CH], y[c][:])
-            nc.vector.tensor_copy(woven(y_bf[c][:]), planar(y[c][:]))
-            if c > 0:
-                quantize_y(c - 1)
-        last = (NCH - 1) * CH
-        nc.sync.dma_start(out_words[:, :last], y_words[:, :last].bitcast(I32))
-        quantize_y(NCH - 1)
-        nc.sync.dma_start(out_words[:, last:], y_words[:, last:].bitcast(I32))
+            second_product(c)
+        copy_y(0)
+        nc.scalar.copy(out=woven(y_bf[0][:]), in_=planar(second[0][:]))
+        copy_y(1)
+        copy_y(2)
+        quantize_y(0)
+        round_y(3, second[3][:])
+        copy_y(3)
+        round_y(1, y[1])
+        quantize_y(3)
+        round_y(2, y[2])
+        quantize_y(1)
+        nc.sync.dma_start(out_words[:, : 2 * CH], y_words[:, : 2 * CH].bitcast(I32))
+        quantize_y(2)
+        nc.sync.dma_start(out_words[:, 2 * CH :], y_words[:, 2 * CH :].bitcast(I32))
         for q in range(4):
             queue = nc.scalar if q % 2 else nc.sync
             queue.dma_start(

@@ -16,14 +16,17 @@ ADD = mybir.AluOpType.add
 
 P = 128
 PACK = 4
+QUADRANTS = 4
 CH = 128
 NCH = S // CH
+W1_VECTOR = 96
+W2_VECTOR = 48
 
 
-def deal(engine_copy, grouped, raw, m0, m1, raw_m0):
+def deal(engine_copy, dealt, raw, m0, m1):
     engine_copy(
-        out=grouped[:, :, m0:m1, :].rearrange("p (u e) m j -> p u m j e", e=2),
-        in_=raw[:, :, PACK * (m0 - raw_m0) : PACK * (m1 - raw_m0)].rearrange("p j (m u e) -> p u m j e", u=2, e=2),
+        out=dealt[:, :, m0:m1, :].rearrange("p (u e) m j -> p u m j e", e=2),
+        in_=raw[:, :, PACK * m0 : PACK * m1].rearrange("p j (m u e) -> p u m j e", u=2, e=2),
     )
 
 
@@ -33,6 +36,10 @@ def woven(tile):
 
 def planar(tile):
     return tile.rearrange("p t (c i) -> p c t i", i=4)
+
+
+def chunk(c):
+    return slice(c * CH, (c + 1) * CH)
 
 
 def tile_picked_posadd_none_po_kernel(
@@ -50,44 +57,43 @@ def tile_picked_posadd_none_po_kernel(
         nc.vector.memset(xs_all[:].bitcast(I32), 0)
         pe_rows = pe.rearrange("(p t) c -> p t c", t=PACK)
         pe_all = [keep.tile([P, T], F32, name=f"pe_all{t}") for t in range(PACK)]
-        nc.sync.dma_start(pe_all[0][:, : T // 2], pe_rows[:, 0, : T // 2])
-        for q in range(4):
+        nc.sync.dma_start(pe_all[0][:], pe_rows[:, 0, :])
+        for q in range(QUADRANTS):
             nc.sync.dma_start(
                 xs_all[32 * q : 32 * q + 4, :].bitcast(I32), x_scales[0, 4 * q : 4 * q + 4, :].bitcast(I32)
             )
-        nc.sync.dma_start(pe_all[0][:, T // 2 :], pe_rows[:, 0, T // 2 :])
-
-        w1_rows = w1.rearrange("(p j) c -> p j c", j=PACK)
-        w1_raw = [keep.tile([P, PACK, H // 2], F32, name=f"w1_raw{u}") for u in range(2)]
-        for t in range(1, PACK - 1):
-            nc.sync.dma_start(pe_all[t][:], pe_rows[:, t, :])
-        for u in range(2):
-            nc.sync.dma_start(w1_raw[u][:], w1_rows[:, :, u * (H // 2) : (u + 1) * (H // 2)])
+        w1_raw = keep.tile([P, PACK, H], F32, name="w1_raw")
+        nc.sync.dma_start(w1_raw[:], w1.rearrange("(p j) c -> p j c", j=PACK))
         xw_all = keep.tile([P, T], U32, name="xw_all", align_bytes=64)
+        nc.sync.dma_start(pe_all[1][:], pe_rows[:, 1, :])
+        nc.sync.dma_start(pe_all[2][:], pe_rows[:, 2, :])
         nc.sync.dma_start(xw_all[:].bitcast(I32), x_words[0].rearrange("p n t -> p (n t)").bitcast(I32))
-        nc.sync.dma_start(pe_all[PACK - 1][:], pe_rows[:, PACK - 1, :])
-        w2_rows = w2.rearrange("(p j) c -> p j c", j=PACK)
-        w2_raw = [keep.tile([P, PACK, H // 2], F32, name=f"w2_raw{u}") for u in range(2)]
-        for u in range(2):
-            nc.sync.dma_start(w2_raw[u][:], w2_rows[:, :, u * (H // 2) : (u + 1) * (H // 2)])
+        nc.sync.dma_start(pe_all[3][:], pe_rows[:, 3, :])
+        w2_raw = keep.tile([P, PACK, H], F32, name="w2_raw")
+        nc.sync.dma_start(w2_raw[:], w2.rearrange("(p j) c -> p j c", j=PACK))
 
-        g = keep.tile([P, PACK, S], F32, name="g")
-        xs = keep.tile([P, S], U8, name="xs", align_bytes=64)
-        nc.vector.tensor_copy(xs[:], xs_all[:].indirect(offsets[:]))
+        pe_picked = keep.tile([P, PACK, S], F32, name="pe_picked")
 
         def gather_pe(t):
-            nc.vector.tensor_copy(g[:, t, :], pe_all[t][:].indirect(offsets[:]))
+            nc.vector.tensor_copy(pe_picked[:, t, :], pe_all[t][:].indirect(offsets[:]))
+
+        gather_pe(0)
+        xs_picked = keep.tile([P, S], U8, name="xs_picked", align_bytes=64)
+        nc.vector.tensor_copy(xs_picked[:], xs_all[:].indirect(offsets[:]))
 
         w1_bf = keep.tile([P, PACK, P, PACK], BF16, name="w1_bf", align_bytes=64)
         w1_words = keep.tile([P, H], U32, name="w1_words", align_bytes=64)
         w1_scales = keep.tile([P, H], U8, name="w1_scales", align_bytes=64)
-        for t in range(PACK - 1):
-            gather_pe(t)
-        deal(nc.scalar.copy, w1_bf, w1_raw[0], 0, P // 2, 0)
-        deal(nc.vector.tensor_copy, w1_bf, w1_raw[1], P // 2, P, P // 2)
+        deal(nc.vector.tensor_copy, w1_bf, w1_raw, 0, W1_VECTOR)
+        deal(nc.scalar.copy, w1_bf, w1_raw, W1_VECTOR, P)
         nc.vector.quantize_mx(
             out=w1_words[:].bitcast(FP8X4), scales=w1_scales[:], in_=w1_bf[:].rearrange("p t m j -> p (t m j)")
         )
+        gather_pe(1)
+        gather_pe(2)
+        xw_picked = keep.tile([P, S], U32, name="xw_picked", align_bytes=64)
+        nc.vector.tensor_copy(xw_picked[:], xw_all[:].indirect(offsets[:]))
+        gather_pe(3)
 
         def product(bank, w_words, w_scales, words, scales):
             for t in range(PACK):
@@ -101,19 +107,16 @@ def tile_picked_posadd_none_po_kernel(
                     stop=True,
                 )
 
-        xw_picked = keep.tile([P, S], U32, name="xw_picked", align_bytes=64)
-        xw = [xw_picked[:, c * CH : (c + 1) * CH] for c in range(NCH)]
-        first = [psum.tile([P, PACK, CH], F32, name=f"first{c}") for c in range(NCH)]
-        nc.vector.tensor_copy(xw_picked[:], xw_all[:].indirect(offsets[:]))
-        gather_pe(PACK - 1)
-        for c in range(NCH):
-            product(first[c], w1_words, w1_scales, xw[c], xs[:, c * CH : (c + 1) * CH])
+        first = []
+
+        def first_product(c):
+            first.append(psum.tile([P, PACK, CH], F32, name=f"first{c}", tag=f"first{c % 2}"))
+            product(first[c], w1_words, w1_scales, xw_picked[:, chunk(c)], xs_picked[:, chunk(c)])
 
         w2_bf = keep.tile([P, PACK, P, PACK], BF16, name="w2_bf", align_bytes=64)
         w2_words = keep.tile([P, H], U32, name="w2_words", align_bytes=64)
         w2_scales = keep.tile([P, H], U8, name="w2_scales", align_bytes=64)
-        for u in range(2):
-            deal(nc.scalar.copy, w2_bf, w2_raw[u], u * P // 2, (u + 1) * P // 2, u * P // 2)
+        deal(nc.scalar.copy, w2_bf, w2_raw, W2_VECTOR, P)
 
         def quantize_w2(u):
             cols = slice(2 * u * P, 2 * (u + 1) * P)
@@ -123,73 +126,78 @@ def tile_picked_posadd_none_po_kernel(
                 in_=w2_bf[:, 2 * u : 2 * u + 2].rearrange("p t m j -> p (t m j)"),
             )
 
-        h_own = [keep.tile([P, CH, PACK], BF16, name=f"h_bf{c}", align_bytes=64) for c in range(NCH - 1)]
-        h_bf = [tile[:] for tile in h_own] + [w2_bf[:, PACK - 1]]
+        h_own = [keep.tile([P, CH, PACK], BF16, name=f"h_bf{c}", align_bytes=64) for c in range(2)]
+        h_bf = [tile[:] for tile in h_own] + [w2_bf[:, 0], w2_bf[:, 1]]
         h_words = [keep.tile([P, CH], U32, name=f"h_words{c}", align_bytes=64) for c in range(NCH)]
         h_scales = [keep.tile([P, CH], U8, name=f"h_scales{c}", align_bytes=64) for c in range(NCH)]
 
         def add(c):
-            nc.vector.tensor_tensor(
-                woven(h_bf[c]), planar(first[c][:]), planar(g[:, :, c * CH : (c + 1) * CH]), ADD
-            )
+            nc.vector.tensor_tensor(woven(h_bf[c]), planar(first[c][:]), planar(pe_picked[:, :, chunk(c)]), ADD)
 
         def quantize_h(c):
             nc.vector.quantize_mx(
                 out=h_words[c][:].bitcast(FP8X4), scales=h_scales[c][:], in_=h_bf[c].rearrange("p n t -> p (n t)")
             )
 
-        second = [psum.tile([P, PACK, CH], F32, name=f"second{c}") for c in range(NCH)]
-        y_tiles = [keep.tile([P, PACK, CH], F32, name=f"y{c}") for c in range(NCH)]
-        y = [tile[:] for tile in y_tiles]
-        y_bf = [keep.tile([P, CH, PACK], BF16, name=f"y_bf{c}", align_bytes=64) for c in range(NCH)]
-        y_words = keep.tile([P, S], U32, name="y_words", align_bytes=64)
-        y_scales = keep.tile([P, S], U8, name="y_scales", align_bytes=64)
-        out_rows = out_0.rearrange("(p t) n -> p t n", t=PACK)
-        out_words = out_1[0].rearrange("p n t -> p (n t)").bitcast(I32)
-
-        def second_product(c):
-            product(second[c], w2_words, w2_scales, h_words[c][:], h_scales[c][:])
-
-        def copy_y(c):
-            nc.scalar.copy(out=y[c], in_=second[c][:])
-            nc.sync.dma_start(out_rows[:, :, c * CH : (c + 1) * CH], y[c])
-
-        def round_y(c, source):
-            nc.vector.tensor_copy(out=woven(y_bf[c][:]), in_=planar(source))
-
-        def quantize_y(c):
-            cols = slice(c * CH, (c + 1) * CH)
-            nc.vector.quantize_mx(
-                out=y_words[:, cols].bitcast(FP8X4), scales=y_scales[:, cols], in_=y_bf[c][:].rearrange("p n t -> p (n t)")
-            )
-
+        first_product(0)
+        first_product(1)
         add(0)
+        first_product(2)
         add(1)
+        first_product(3)
         quantize_h(0)
-        add(2)
         quantize_h(1)
+        deal(nc.vector.tensor_copy, w2_bf, w2_raw, 0, W2_VECTOR)
         quantize_w2(0)
         quantize_w2(1)
+        add(2)
         add(3)
         quantize_h(2)
         quantize_h(3)
+
+        second = [psum.tile([P, PACK, CH], F32, name=f"second{c}") for c in range(NCH)]
         for c in range(NCH):
-            second_product(c)
-        copy_y(0)
-        nc.scalar.copy(out=woven(y_bf[0][:]), in_=planar(second[0][:]))
-        copy_y(1)
-        copy_y(2)
+            product(second[c], w2_words, w2_scales, h_words[c][:], h_scales[c][:])
+
+        y_front = [keep.tile([P, PACK, CH], F32, name=f"y_front{c}") for c in range(2)]
+        y_back = keep.tile([P, PACK, 2 * CH], F32, name="y_back")
+        y = [tile[:] for tile in y_front] + [y_back[:, :, :CH], y_back[:, :, CH:]]
+        out_rows = out_0.rearrange("(p t) n -> p t n", t=PACK)
+        for c in range(2):
+            nc.scalar.copy(out=y[c], in_=second[c][:])
+            nc.sync.dma_start(out_rows[:, :, chunk(c)], y[c])
+        for c in range(2, NCH):
+            nc.scalar.copy(out=y[c], in_=second[c][:])
+        nc.sync.dma_start(out_rows[:, :, 2 * CH :], y_back[:])
+
+        y_bf = [keep.tile([P, CH, PACK], BF16, name=f"y_bf{c}", align_bytes=64) for c in range(NCH)]
+        y_words = keep.tile([P, S], U32, name="y_words", align_bytes=64)
+        y_scales = keep.tile([P, S], U8, name="y_scales", align_bytes=64)
+        out_words = out_1[0].rearrange("p n t -> p (n t)").bitcast(I32)
+
+        def round_y(c, tokens):
+            nc.vector.tensor_copy(out=woven(y_bf[c][:, :tokens, :]), in_=planar(y[c][:, :, :tokens]))
+
+        def quantize_y(c):
+            nc.vector.quantize_mx(
+                out=y_words[:, chunk(c)].bitcast(FP8X4),
+                scales=y_scales[:, chunk(c)],
+                in_=y_bf[c][:].rearrange("p n t -> p (n t)"),
+            )
+
+        last, half = NCH - 1, CH // 2
+        nc.scalar.copy(out=woven(y_bf[last][:, half:, :]), in_=planar(second[last][:, :, half:]))
+        round_y(0, CH)
+        round_y(1, CH)
         quantize_y(0)
-        round_y(3, second[3][:])
-        copy_y(3)
-        round_y(1, y[1])
-        quantize_y(3)
-        round_y(2, y[2])
+        round_y(2, CH)
         quantize_y(1)
-        nc.sync.dma_start(out_words[:, : 2 * CH], y_words[:, : 2 * CH].bitcast(I32))
+        round_y(last, half)
         quantize_y(2)
-        nc.sync.dma_start(out_words[:, 2 * CH :], y_words[:, 2 * CH :].bitcast(I32))
-        for q in range(4):
+        nc.sync.dma_start(out_words[:, : last * CH], y_words[:, : last * CH].bitcast(I32))
+        quantize_y(last)
+        nc.sync.dma_start(out_words[:, last * CH :], y_words[:, last * CH :].bitcast(I32))
+        for q in range(QUADRANTS):
             queue = nc.scalar if q % 2 else nc.sync
             queue.dma_start(
                 out_2[0, 4 * q : 4 * q + 4, :].bitcast(I32), y_scales[32 * q : 32 * q + 4, :].bitcast(I32)

@@ -19,14 +19,16 @@ PACK = 4
 QUADRANTS = 4
 CH = 128
 NCH = S // CH
-W1_VECTOR = 96
-W2_VECTOR = 48
+HALF = S // 2
+WH = P // 2
+W1_VECTOR = 36
+LAST_VECTOR = 64
 
 
-def deal(engine_copy, dealt, raw, m0, m1):
+def deal(engine_copy, dealt, raw, base, m0, m1, u0, u1):
     engine_copy(
-        out=dealt[:, :, m0:m1, :].rearrange("p (u e) m j -> p u m j e", e=2),
-        in_=raw[:, :, PACK * m0 : PACK * m1].rearrange("p j (m u e) -> p u m j e", u=2, e=2),
+        out=dealt[:, 2 * u0 : 2 * u1, base + m0 : base + m1, :].rearrange("p (u e) m j -> p u m j e", e=2),
+        in_=raw[:, :, PACK * m0 : PACK * m1].rearrange("p j (m u e) -> p u m j e", u=2, e=2)[:, u0:u1],
     )
 
 
@@ -40,6 +42,10 @@ def planar(tile):
 
 def chunk(c):
     return slice(c * CH, (c + 1) * CH)
+
+
+def half(h):
+    return slice(h * HALF, (h + 1) * HALF)
 
 
 def tile_picked_posadd_none_po_kernel(
@@ -62,15 +68,19 @@ def tile_picked_posadd_none_po_kernel(
             nc.sync.dma_start(
                 xs_all[32 * q : 32 * q + 4, :].bitcast(I32), x_scales[0, 4 * q : 4 * q + 4, :].bitcast(I32)
             )
-        w1_raw = keep.tile([P, PACK, H], F32, name="w1_raw")
-        nc.sync.dma_start(w1_raw[:], w1.rearrange("(p j) c -> p j c", j=PACK))
+        w1_rows = w1.rearrange("(p j) c -> p j c", j=PACK)
+        w2_rows = w2.rearrange("(p j) c -> p j c", j=PACK)
+        w1_raw = [keep.tile([P, PACK, H // 2], F32, name=f"w1_raw{a}") for a in range(2)]
+        w2_raw = [keep.tile([P, PACK, H // 2], F32, name=f"w2_raw{a}", tag=f"w2_raw{a}", align_bytes=64) for a in range(2)]
         xw_all = keep.tile([P, T], U32, name="xw_all", align_bytes=64)
+        nc.sync.dma_start(w1_raw[0][:], w1_rows[:, :, half(0)])
         nc.sync.dma_start(pe_all[1][:], pe_rows[:, 1, :])
-        nc.sync.dma_start(pe_all[2][:], pe_rows[:, 2, :])
         nc.sync.dma_start(xw_all[:].bitcast(I32), x_words[0].rearrange("p n t -> p (n t)").bitcast(I32))
+        nc.sync.dma_start(w1_raw[1][:], w1_rows[:, :, half(1)])
+        nc.sync.dma_start(pe_all[2][:], pe_rows[:, 2, :])
         nc.sync.dma_start(pe_all[3][:], pe_rows[:, 3, :])
-        w2_raw = keep.tile([P, PACK, H], F32, name="w2_raw")
-        nc.sync.dma_start(w2_raw[:], w2.rearrange("(p j) c -> p j c", j=PACK))
+        for a in range(2):
+            nc.sync.dma_start(w2_raw[a][:], w2_rows[:, :, half(a)])
 
         pe_picked = keep.tile([P, PACK, S], F32, name="pe_picked")
 
@@ -84,39 +94,44 @@ def tile_picked_posadd_none_po_kernel(
         w1_bf = keep.tile([P, PACK, P, PACK], BF16, name="w1_bf", align_bytes=64)
         w1_words = keep.tile([P, H], U32, name="w1_words", align_bytes=64)
         w1_scales = keep.tile([P, H], U8, name="w1_scales", align_bytes=64)
-        deal(nc.vector.tensor_copy, w1_bf, w1_raw, 0, W1_VECTOR)
-        deal(nc.scalar.copy, w1_bf, w1_raw, W1_VECTOR, P)
+        deal(nc.scalar.copy, w1_bf, w1_raw[0], 0, 0, WH, 0, 2)
+        gather_pe(1)
+        xw_picked = keep.tile([P, S], U32, name="xw_picked", align_bytes=64)
+        nc.vector.tensor_copy(xw_picked[:], xw_all[:].indirect(offsets[:]))
+        deal(nc.vector.tensor_copy, w1_bf, w1_raw[1], WH, 0, W1_VECTOR, 0, 2)
+        deal(nc.scalar.copy, w1_bf, w1_raw[1], WH, W1_VECTOR, WH, 0, 2)
         nc.vector.quantize_mx(
             out=w1_words[:].bitcast(FP8X4), scales=w1_scales[:], in_=w1_bf[:].rearrange("p t m j -> p (t m j)")
         )
-        gather_pe(1)
         gather_pe(2)
-        xw_picked = keep.tile([P, S], U32, name="xw_picked", align_bytes=64)
-        nc.vector.tensor_copy(xw_picked[:], xw_all[:].indirect(offsets[:]))
-        gather_pe(3)
+        for h in range(2):
+            nc.vector.tensor_copy(
+                pe_picked[:, 3, half(h)], pe_all[3][:].indirect(offsets[:, h * HALF // 16 : (h + 1) * HALF // 16])
+            )
 
-        def product(bank, w_words, w_scales, words, scales):
-            for t in range(PACK):
-                nc.tensor.matmul_mx(
-                    out=bank[:, t, :],
-                    lhsT=w_words[:, t * P : (t + 1) * P].bitcast(FP8X4),
-                    lhsT_scale=w_scales[:, t * P : (t + 1) * P],
-                    rhs=words.bitcast(FP8X4),
-                    rhs_scale=scales,
-                    start=True,
-                    stop=True,
-                )
+        def product(out, t, w_words, w_scales, words, scales):
+            nc.tensor.matmul_mx(
+                out=out,
+                lhsT=w_words[:, t * P : (t + 1) * P].bitcast(FP8X4),
+                lhsT_scale=w_scales[:, t * P : (t + 1) * P],
+                rhs=words.bitcast(FP8X4),
+                rhs_scale=scales,
+                start=True,
+                stop=True,
+            )
 
         first = []
 
         def first_product(c):
             first.append(psum.tile([P, PACK, CH], F32, name=f"first{c}", tag=f"first{c % 2}"))
-            product(first[c], w1_words, w1_scales, xw_picked[:, chunk(c)], xs_picked[:, chunk(c)])
+            for t in range(PACK):
+                product(first[c][:, t, :], t, w1_words, w1_scales, xw_picked[:, chunk(c)], xs_picked[:, chunk(c)])
 
         w2_bf = keep.tile([P, PACK, P, PACK], BF16, name="w2_bf", align_bytes=64)
         w2_words = keep.tile([P, H], U32, name="w2_words", align_bytes=64)
         w2_scales = keep.tile([P, H], U8, name="w2_scales", align_bytes=64)
-        deal(nc.scalar.copy, w2_bf, w2_raw, W2_VECTOR, P)
+        for a in range(2):
+            deal(nc.scalar.copy, w2_bf, w2_raw[a], a * WH, 0, WH, 0, 2)
 
         def quantize_w2(u):
             cols = slice(2 * u * P, 2 * (u + 1) * P)
@@ -126,17 +141,22 @@ def tile_picked_posadd_none_po_kernel(
                 in_=w2_bf[:, 2 * u : 2 * u + 2].rearrange("p t m j -> p (t m j)"),
             )
 
-        h_own = [keep.tile([P, CH, PACK], BF16, name=f"h_bf{c}", align_bytes=64) for c in range(2)]
-        h_bf = [tile[:] for tile in h_own] + [w2_bf[:, 0], w2_bf[:, 1]]
-        h_words = [keep.tile([P, CH], U32, name=f"h_words{c}", align_bytes=64) for c in range(NCH)]
-        h_scales = [keep.tile([P, CH], U8, name=f"h_scales{c}", align_bytes=64) for c in range(NCH)]
+        h_front = keep.tile([P, HALF, PACK], BF16, name="h_front", align_bytes=64)
+        h_third = keep.tile([P, CH, PACK], BF16, name="h_third", align_bytes=64)
+        h_bf = [h_front[:, :CH], h_front[:, CH:], h_third[:], w2_bf[:, 0]]
+        widths = (HALF, CH, CH)
+        tags = ("h_words0", "w2_raw1", "h_words2")
+        h_words = [
+            keep.tile([P, n], U32, name=f"h_words{i}", tag=tags[i], align_bytes=64) for i, n in enumerate(widths)
+        ]
+        h_scales = [keep.tile([P, n], U8, name=f"h_scales{i}", align_bytes=64) for i, n in enumerate(widths)]
 
         def add(c):
             nc.vector.tensor_tensor(woven(h_bf[c]), planar(first[c][:]), planar(pe_picked[:, :, chunk(c)]), ADD)
 
-        def quantize_h(c):
+        def quantize_h(i, values):
             nc.vector.quantize_mx(
-                out=h_words[c][:].bitcast(FP8X4), scales=h_scales[c][:], in_=h_bf[c].rearrange("p n t -> p (n t)")
+                out=h_words[i][:].bitcast(FP8X4), scales=h_scales[i][:], in_=values.rearrange("p n t -> p (n t)")
             )
 
         first_product(0)
@@ -145,58 +165,55 @@ def tile_picked_posadd_none_po_kernel(
         first_product(2)
         add(1)
         first_product(3)
-        quantize_h(0)
-        quantize_h(1)
-        deal(nc.vector.tensor_copy, w2_bf, w2_raw, 0, W2_VECTOR)
+        add(2)
+        quantize_h(0, h_front[:])
         quantize_w2(0)
         quantize_w2(1)
-        add(2)
         add(3)
-        quantize_h(2)
-        quantize_h(3)
+        quantize_h(1, h_bf[2])
+        quantize_h(2, h_bf[3])
 
-        second = [psum.tile([P, PACK, CH], F32, name=f"second{c}") for c in range(NCH)]
-        for c in range(NCH):
-            product(second[c], w2_words, w2_scales, h_words[c][:], h_scales[c][:])
-
-        y_front = [keep.tile([P, PACK, CH], F32, name=f"y_front{c}") for c in range(2)]
-        y_back = keep.tile([P, PACK, 2 * CH], F32, name="y_back")
-        y = [tile[:] for tile in y_front] + [y_back[:, :, :CH], y_back[:, :, CH:]]
         out_rows = out_0.rearrange("(p t) n -> p t n", t=PACK)
-        for c in range(2):
-            nc.scalar.copy(out=y[c], in_=second[c][:])
-            nc.sync.dma_start(out_rows[:, :, chunk(c)], y[c])
+        out_words = out_1[0].rearrange("p n t -> p (n t)").bitcast(I32)
+        y_front = keep.tile([P, PACK, HALF], F32, name="y_front")
+        for u in range(2):
+            bank = psum.tile([P, 2, HALF], F32, name=f"front{u}")
+            for e in range(2):
+                product(bank[:, e, :], 2 * u + e, w2_words, w2_scales, h_words[0][:], h_scales[0][:])
+            nc.scalar.copy(out=y_front[:, 2 * u : 2 * u + 2, :], in_=bank[:])
+            nc.sync.dma_start(out_rows[:, 2 * u : 2 * u + 2, half(0)], y_front[:, 2 * u : 2 * u + 2, :])
+        back = []
+        y_back = []
         for c in range(2, NCH):
-            nc.scalar.copy(out=y[c], in_=second[c][:])
-        nc.sync.dma_start(out_rows[:, :, 2 * CH :], y_back[:])
+            bank = psum.tile([P, PACK, CH], F32, name=f"back{c}")
+            back.append(bank)
+            for t in range(PACK):
+                product(bank[:, t, :], t, w2_words, w2_scales, h_words[c - 1][:], h_scales[c - 1][:])
+            y_back.append(keep.tile([P, PACK, CH], F32, name=f"y_back{c}"))
+            nc.scalar.copy(out=y_back[-1][:], in_=bank[:])
+            nc.sync.dma_start(out_rows[:, :, chunk(c)], y_back[-1][:])
 
-        y_bf = [keep.tile([P, CH, PACK], BF16, name=f"y_bf{c}", align_bytes=64) for c in range(NCH)]
+        y_bf = [keep.tile([P, n, PACK], BF16, name=f"y_bf{i}", align_bytes=64) for i, n in enumerate(widths)]
         y_words = keep.tile([P, S], U32, name="y_words", align_bytes=64)
         y_scales = keep.tile([P, S], U8, name="y_scales", align_bytes=64)
-        out_words = out_1[0].rearrange("p n t -> p (n t)").bitcast(I32)
 
-        def round_y(c, tokens):
-            nc.vector.tensor_copy(out=woven(y_bf[c][:, :tokens, :]), in_=planar(y[c][:, :, :tokens]))
-
-        def quantize_y(c):
+        def quantize_y(i, tokens):
             nc.vector.quantize_mx(
-                out=y_words[:, chunk(c)].bitcast(FP8X4),
-                scales=y_scales[:, chunk(c)],
-                in_=y_bf[c][:].rearrange("p n t -> p (n t)"),
+                out=y_words[:, tokens].bitcast(FP8X4),
+                scales=y_scales[:, tokens],
+                in_=y_bf[i][:].rearrange("p n t -> p (n t)"),
             )
 
-        last, half = NCH - 1, CH // 2
-        nc.scalar.copy(out=woven(y_bf[last][:, half:, :]), in_=planar(second[last][:, :, half:]))
-        round_y(0, CH)
-        round_y(1, CH)
-        quantize_y(0)
-        round_y(2, CH)
-        quantize_y(1)
-        round_y(last, half)
-        quantize_y(2)
-        nc.sync.dma_start(out_words[:, : last * CH], y_words[:, : last * CH].bitcast(I32))
-        quantize_y(last)
-        nc.sync.dma_start(out_words[:, last * CH :], y_words[:, last * CH :].bitcast(I32))
+        v = LAST_VECTOR
+        nc.scalar.copy(out=woven(y_bf[2][:, v:, :]), in_=planar(back[1][:, :, v:]))
+        nc.vector.tensor_copy(out=woven(y_bf[0][:]), in_=planar(y_front[:]))
+        nc.vector.tensor_copy(out=woven(y_bf[1][:]), in_=planar(y_back[0][:]))
+        quantize_y(0, half(0))
+        nc.sync.dma_start(out_words[:, half(0)], y_words[:, half(0)].bitcast(I32))
+        nc.vector.tensor_copy(out=woven(y_bf[2][:, :v, :]), in_=planar(y_back[1][:, :, :v]))
+        quantize_y(1, chunk(2))
+        quantize_y(2, chunk(3))
+        nc.sync.dma_start(out_words[:, half(1)], y_words[:, half(1)].bitcast(I32))
         for q in range(QUADRANTS):
             queue = nc.scalar if q % 2 else nc.sync
             queue.dma_start(

@@ -22,7 +22,7 @@ NCH = S // CH
 HALF = S // 2
 WH = P // 2
 W1_VECTOR = 36
-LAST_VECTOR = 64
+LAST_VECTOR = 32
 
 
 def deal(engine_copy, dealt, raw, base, m0, m1, u0, u1):
@@ -33,11 +33,11 @@ def deal(engine_copy, dealt, raw, base, m0, m1, u0, u1):
 
 
 def woven(tile):
-    return tile.rearrange("p (c i) t -> p c t i", i=4)
+    return tile.rearrange("p (c i) t -> p c t i", i=2)
 
 
 def planar(tile):
-    return tile.rearrange("p t (c i) -> p c t i", i=4)
+    return tile.rearrange("p t (c i) -> p c t i", i=2)
 
 
 def chunk(c):
@@ -73,8 +73,8 @@ def tile_picked_posadd_none_po_kernel(
         w1_raw = [keep.tile([P, PACK, H // 2], F32, name=f"w1_raw{a}") for a in range(2)]
         w2_raw = [keep.tile([P, PACK, H // 2], F32, name=f"w2_raw{a}", tag=f"w2_raw{a}", align_bytes=64) for a in range(2)]
         xw_all = keep.tile([P, T], U32, name="xw_all", align_bytes=64)
-        nc.sync.dma_start(w1_raw[0][:], w1_rows[:, :, half(0)])
         nc.sync.dma_start(pe_all[1][:], pe_rows[:, 1, :])
+        nc.sync.dma_start(w1_raw[0][:], w1_rows[:, :, half(0)])
         nc.sync.dma_start(xw_all[:].bitcast(I32), x_words[0].rearrange("p n t -> p (n t)").bitcast(I32))
         nc.sync.dma_start(w1_raw[1][:], w1_rows[:, :, half(1)])
         nc.sync.dma_start(pe_all[2][:], pe_rows[:, 2, :])
@@ -130,20 +130,21 @@ def tile_picked_posadd_none_po_kernel(
         w2_bf = keep.tile([P, PACK, P, PACK], BF16, name="w2_bf", align_bytes=64)
         w2_words = keep.tile([P, H], U32, name="w2_words", align_bytes=64)
         w2_scales = keep.tile([P, H], U8, name="w2_scales", align_bytes=64)
-        for a in range(2):
-            deal(nc.scalar.copy, w2_bf, w2_raw[a], a * WH, 0, WH, 0, 2)
+        deal(nc.scalar.copy, w2_bf, w2_raw[0], 0, 0, WH, 0, 2)
+        for u in range(2):
+            deal(nc.scalar.copy, w2_bf, w2_raw[1], WH, 0, WH, u, u + 1)
 
-        def quantize_w2(u):
-            cols = slice(2 * u * P, 2 * (u + 1) * P)
+        def quantize_w2(t):
+            cols = slice(t * P, (t + 1) * P)
             nc.vector.quantize_mx(
                 out=w2_words[:, cols].bitcast(FP8X4),
                 scales=w2_scales[:, cols],
-                in_=w2_bf[:, 2 * u : 2 * u + 2].rearrange("p t m j -> p (t m j)"),
+                in_=w2_bf[:, t].rearrange("p m j -> p (m j)"),
             )
 
         h_front = keep.tile([P, HALF, PACK], BF16, name="h_front", align_bytes=64)
         h_third = keep.tile([P, CH, PACK], BF16, name="h_third", align_bytes=64)
-        h_bf = [h_front[:, :CH], h_front[:, CH:], h_third[:], w2_bf[:, 0]]
+        h_bf = [h_front[:, :CH], h_front[:, CH:], h_third[:], w2_bf[:, 2]]
         widths = (HALF, CH, CH)
         tags = ("h_words0", "w2_raw1", "h_words2")
         h_words = [
@@ -167,8 +168,8 @@ def tile_picked_posadd_none_po_kernel(
         first_product(3)
         add(2)
         quantize_h(0, h_front[:])
-        quantize_w2(0)
-        quantize_w2(1)
+        for t in range(PACK):
+            quantize_w2(t)
         add(3)
         quantize_h(1, h_bf[2])
         quantize_h(2, h_bf[3])

@@ -22,7 +22,7 @@ NCH = S // CH
 HALF = S // 2
 WH = P // 2
 W1_VECTOR = 36
-LAST_VECTOR = 32
+LAST_VECTOR = 48
 
 
 def deal(engine_copy, dealt, raw, base, m0, m1, u0, u1):
@@ -143,8 +143,7 @@ def tile_picked_posadd_none_po_kernel(
             )
 
         h_front = keep.tile([P, HALF, PACK], BF16, name="h_front", align_bytes=64)
-        h_third = keep.tile([P, CH, PACK], BF16, name="h_third", align_bytes=64)
-        h_bf = [h_front[:, :CH], h_front[:, CH:], h_third[:], w2_bf[:, 2]]
+        h_bf = [h_front[:, :CH], h_front[:, CH:], w2_bf[:, 0], w2_bf[:, 2]]
         widths = (HALF, CH, CH)
         tags = ("h_words0", "w2_raw1", "h_words2")
         h_words = [
@@ -166,12 +165,19 @@ def tile_picked_posadd_none_po_kernel(
         first_product(2)
         add(1)
         first_product(3)
+        for c in range(2):
+            nc.vector.quantize_mx(
+                out=h_words[0][:, chunk(c)].bitcast(FP8X4),
+                scales=h_scales[0][:, chunk(c)],
+                in_=h_bf[c].rearrange("p n t -> p (n t)"),
+            )
+        quantize_w2(0)
+        quantize_w2(1)
         add(2)
-        quantize_h(0, h_front[:])
-        for t in range(PACK):
-            quantize_w2(t)
-        add(3)
+        quantize_w2(2)
+        quantize_w2(3)
         quantize_h(1, h_bf[2])
+        add(3)
         quantize_h(2, h_bf[3])
 
         out_rows = out_0.rearrange("(p t) n -> p t n", t=PACK)
@@ -194,7 +200,7 @@ def tile_picked_posadd_none_po_kernel(
             nc.scalar.copy(out=y_back[-1][:], in_=bank[:])
             nc.sync.dma_start(out_rows[:, :, chunk(c)], y_back[-1][:])
 
-        y_bf = [keep.tile([P, n, PACK], BF16, name=f"y_bf{i}", align_bytes=64) for i, n in enumerate(widths)]
+        y_bf = [keep.tile([P, HALF, PACK], BF16, name=f"y_bf{i}", align_bytes=64) for i in range(2)]
         y_words = keep.tile([P, S], U32, name="y_words", align_bytes=64)
         y_scales = keep.tile([P, S], U8, name="y_scales", align_bytes=64)
 
@@ -206,14 +212,13 @@ def tile_picked_posadd_none_po_kernel(
             )
 
         v = LAST_VECTOR
-        nc.scalar.copy(out=woven(y_bf[2][:, v:, :]), in_=planar(back[1][:, :, v:]))
+        nc.scalar.copy(out=woven(y_bf[1][:, CH + v :, :]), in_=planar(back[1][:, :, v:]))
         nc.vector.tensor_copy(out=woven(y_bf[0][:]), in_=planar(y_front[:]))
-        nc.vector.tensor_copy(out=woven(y_bf[1][:]), in_=planar(y_back[0][:]))
+        nc.vector.tensor_copy(out=woven(y_bf[1][:, :CH, :]), in_=planar(y_back[0][:]))
         quantize_y(0, half(0))
         nc.sync.dma_start(out_words[:, half(0)], y_words[:, half(0)].bitcast(I32))
-        nc.vector.tensor_copy(out=woven(y_bf[2][:, :v, :]), in_=planar(y_back[1][:, :, :v]))
-        quantize_y(1, chunk(2))
-        quantize_y(2, chunk(3))
+        nc.vector.tensor_copy(out=woven(y_bf[1][:, CH : CH + v, :]), in_=planar(y_back[1][:, :, :v]))
+        quantize_y(1, half(1))
         nc.sync.dma_start(out_words[:, half(1)], y_words[:, half(1)].bitcast(I32))
         for q in range(QUADRANTS):
             queue = nc.scalar if q % 2 else nc.sync

@@ -22,7 +22,6 @@ NCH = S // CH
 HALF = S // 2
 WH = P // 2
 W1_VECTOR = 36
-LAST_VECTOR = 48
 
 
 def deal(engine_copy, dealt, raw, base, m0, m1, u0, u1):
@@ -57,13 +56,13 @@ def tile_picked_posadd_none_po_kernel(
         psum = ctx.enter_context(tc.psum_pool(name="psum", bufs=1))
 
         offsets = keep.tile([P, S // 16], U16, name="offsets")
-        nc.sync.dma_start(offsets[:], offs)
 
         xs_all = keep.tile([P, T], U8, name="xs_all", align_bytes=64)
         nc.vector.memset(xs_all[:].bitcast(I32), 0)
         pe_rows = pe.rearrange("(p t) c -> p t c", t=PACK)
         pe_all = [keep.tile([P, T], F32, name=f"pe_all{t}") for t in range(PACK)]
         nc.sync.dma_start(pe_all[0][:], pe_rows[:, 0, :])
+        nc.sync.dma_start(offsets[:], offs)
         for q in range(QUADRANTS):
             nc.sync.dma_start(
                 xs_all[32 * q : 32 * q + 4, :].bitcast(I32), x_scales[0, 4 * q : 4 * q + 4, :].bitcast(I32)
@@ -200,7 +199,7 @@ def tile_picked_posadd_none_po_kernel(
             nc.scalar.copy(out=y_back[-1][:], in_=bank[:])
             nc.sync.dma_start(out_rows[:, :, chunk(c)], y_back[-1][:])
 
-        y_bf = [keep.tile([P, HALF, PACK], BF16, name=f"y_bf{i}", align_bytes=64) for i in range(2)]
+        y_bf = [keep.tile([P, n, PACK], BF16, name=f"y_bf{i}", align_bytes=64) for i, n in enumerate(widths)]
         y_words = keep.tile([P, S], U32, name="y_words", align_bytes=64)
         y_scales = keep.tile([P, S], U8, name="y_scales", align_bytes=64)
 
@@ -211,15 +210,14 @@ def tile_picked_posadd_none_po_kernel(
                 in_=y_bf[i][:].rearrange("p n t -> p (n t)"),
             )
 
-        v = LAST_VECTOR
-        nc.scalar.copy(out=woven(y_bf[1][:, CH + v :, :]), in_=planar(back[1][:, :, v:]))
+        nc.scalar.copy(out=woven(y_bf[2][:]), in_=planar(back[1][:]))
         nc.vector.tensor_copy(out=woven(y_bf[0][:]), in_=planar(y_front[:]))
-        nc.vector.tensor_copy(out=woven(y_bf[1][:, :CH, :]), in_=planar(y_back[0][:]))
+        nc.vector.tensor_copy(out=woven(y_bf[1][:]), in_=planar(y_back[0][:]))
         quantize_y(0, half(0))
-        nc.sync.dma_start(out_words[:, half(0)], y_words[:, half(0)].bitcast(I32))
-        nc.vector.tensor_copy(out=woven(y_bf[1][:, CH : CH + v, :]), in_=planar(y_back[1][:, :, :v]))
-        quantize_y(1, half(1))
-        nc.sync.dma_start(out_words[:, half(1)], y_words[:, half(1)].bitcast(I32))
+        quantize_y(1, chunk(2))
+        nc.sync.dma_start(out_words[:, : 3 * CH], y_words[:, : 3 * CH].bitcast(I32))
+        quantize_y(2, chunk(3))
+        nc.sync.dma_start(out_words[:, chunk(3)], y_words[:, chunk(3)].bitcast(I32))
         for q in range(QUADRANTS):
             queue = nc.scalar if q % 2 else nc.sync
             queue.dma_start(

@@ -219,7 +219,6 @@ def tile_picked_posadd_none_po_kernel(
         quantize_y(2, chunk(3))
         nc.sync.dma_start(out_words[:, chunk(3)], y_words[:, chunk(3)].bitcast(I32))
         for q in range(QUADRANTS):
-            queue = nc.scalar if q % 2 else nc.sync
-            queue.dma_start(
+            nc.sync.dma_start(
                 out_2[0, 4 * q : 4 * q + 4, :].bitcast(I32), y_scales[32 * q : 32 * q + 4, :].bitcast(I32)
             )

@@ -13,22 +13,18 @@ U16 = mybir.dt.uint16
 U8 = mybir.dt.uint8
 FP8X4 = mybir.dt.float8_e4m3fn_x4
 ADD = mybir.AluOpType.add
+COPY = mybir.ActivationFunctionType.Copy
 
 P = 128
 PACK = 4
 QUADRANTS = 4
+LIST_ROWS = 16
 CH = 128
 NCH = S // CH
+LAST = NCH - 1
 HALF = S // 2
 WH = P // 2
-W1_VECTOR = 36
-
-
-def deal(engine_copy, dealt, raw, base, m0, m1, u0, u1):
-    engine_copy(
-        out=dealt[:, 2 * u0 : 2 * u1, base + m0 : base + m1, :].rearrange("p (u e) m j -> p u m j e", e=2),
-        in_=raw[:, :, PACK * m0 : PACK * m1].rearrange("p j (m u e) -> p u m j e", u=2, e=2)[:, u0:u1],
-    )
+W2_VECTOR = (40, 24)
 
 
 def woven(tile):
@@ -43,8 +39,12 @@ def chunk(c):
     return slice(c * CH, (c + 1) * CH)
 
 
-def half(h):
-    return slice(h * HALF, (h + 1) * HALF)
+def half(a):
+    return slice(a * HALF, (a + 1) * HALF)
+
+
+def pair(u):
+    return slice(2 * u, 2 * u + 2)
 
 
 def tile_picked_posadd_none_po_kernel(
@@ -55,13 +55,11 @@ def tile_picked_posadd_none_po_kernel(
         keep = ctx.enter_context(tc.tile_pool(name="keep", bufs=1))
         psum = ctx.enter_context(tc.psum_pool(name="psum", bufs=1))
 
-        offsets = keep.tile([P, S // 16], U16, name="offsets")
-
+        offsets = keep.tile([P, S // LIST_ROWS], U16, name="offsets")
         xs_all = keep.tile([P, T], U8, name="xs_all", align_bytes=64)
         nc.vector.memset(xs_all[:].bitcast(I32), 0)
-        pe_rows = pe.rearrange("(p t) c -> p t c", t=PACK)
-        pe_all = [keep.tile([P, T], F32, name=f"pe_all{t}") for t in range(PACK)]
-        nc.sync.dma_start(pe_all[0][:], pe_rows[:, 0, :])
+        xw_all = keep.tile([P, T], U32, name="xw_all", align_bytes=64)
+        nc.sync.dma_start(xw_all[:].bitcast(I32), x_words[0].rearrange("p n t -> p (n t)").bitcast(I32))
         nc.sync.dma_start(offsets[:], offs)
         for q in range(QUADRANTS):
             nc.sync.dma_start(
@@ -69,44 +67,36 @@ def tile_picked_posadd_none_po_kernel(
             )
         w1_rows = w1.rearrange("(p j) c -> p j c", j=PACK)
         w2_rows = w2.rearrange("(p j) c -> p j c", j=PACK)
+        pe_rows = pe.rearrange("(p t) c -> p t c", t=PACK)
         w1_raw = [keep.tile([P, PACK, H // 2], F32, name=f"w1_raw{a}") for a in range(2)]
-        w2_raw = [keep.tile([P, PACK, H // 2], F32, name=f"w2_raw{a}", tag=f"w2_raw{a}", align_bytes=64) for a in range(2)]
-        xw_all = keep.tile([P, T], U32, name="xw_all", align_bytes=64)
-        nc.sync.dma_start(pe_all[1][:], pe_rows[:, 1, :])
-        nc.sync.dma_start(w1_raw[0][:], w1_rows[:, :, half(0)])
-        nc.sync.dma_start(xw_all[:].bitcast(I32), x_words[0].rearrange("p n t -> p (n t)").bitcast(I32))
-        nc.sync.dma_start(w1_raw[1][:], w1_rows[:, :, half(1)])
-        nc.sync.dma_start(pe_all[2][:], pe_rows[:, 2, :])
-        nc.sync.dma_start(pe_all[3][:], pe_rows[:, 3, :])
+        w2_raw = [keep.tile([P, PACK, H // 2], F32, name=f"w2_raw{a}") for a in range(2)]
+        pe_all = [keep.tile([P, T], F32, name=f"pe_all{t}") for t in range(PACK)]
+        for a in range(2):
+            nc.sync.dma_start(w1_raw[a][:], w1_rows[:, :, half(a)])
+        for t in range(PACK):
+            nc.sync.dma_start(pe_all[t][:], pe_rows[:, t, :])
         for a in range(2):
             nc.sync.dma_start(w2_raw[a][:], w2_rows[:, :, half(a)])
 
-        pe_picked = keep.tile([P, PACK, S], F32, name="pe_picked")
+        def entries(tokens):
+            return offsets[:, tokens.start // LIST_ROWS : tokens.stop // LIST_ROWS]
 
-        def gather_pe(t):
-            nc.vector.tensor_copy(pe_picked[:, t, :], pe_all[t][:].indirect(offsets[:]))
-
-        gather_pe(0)
+        xw_picked = keep.tile([P, S], U32, name="xw_picked", align_bytes=64)
+        nc.vector.tensor_copy(xw_picked[:], xw_all[:].indirect(offsets[:]))
         xs_picked = keep.tile([P, S], U8, name="xs_picked", align_bytes=64)
         nc.vector.tensor_copy(xs_picked[:], xs_all[:].indirect(offsets[:]))
 
         w1_bf = keep.tile([P, PACK, P, PACK], BF16, name="w1_bf", align_bytes=64)
         w1_words = keep.tile([P, H], U32, name="w1_words", align_bytes=64)
         w1_scales = keep.tile([P, H], U8, name="w1_scales", align_bytes=64)
-        deal(nc.scalar.copy, w1_bf, w1_raw[0], 0, 0, WH, 0, 2)
-        gather_pe(1)
-        xw_picked = keep.tile([P, S], U32, name="xw_picked", align_bytes=64)
-        nc.vector.tensor_copy(xw_picked[:], xw_all[:].indirect(offsets[:]))
-        deal(nc.vector.tensor_copy, w1_bf, w1_raw[1], WH, 0, W1_VECTOR, 0, 2)
-        deal(nc.scalar.copy, w1_bf, w1_raw[1], WH, W1_VECTOR, WH, 0, 2)
-        nc.vector.quantize_mx(
-            out=w1_words[:].bitcast(FP8X4), scales=w1_scales[:], in_=w1_bf[:].rearrange("p t m j -> p (t m j)")
-        )
-        gather_pe(2)
-        for h in range(2):
-            nc.vector.tensor_copy(
-                pe_picked[:, 3, half(h)], pe_all[3][:].indirect(offsets[:, h * HALF // 16 : (h + 1) * HALF // 16])
+        for a, engine_copy in enumerate((nc.scalar.copy, nc.vector.tensor_copy)):
+            engine_copy(
+                out=w1_bf[:, :, a * WH : (a + 1) * WH, :].rearrange("p (u e) c j -> p u c j e", e=2),
+                in_=w1_raw[a][:].rearrange("p j (c u e) -> p u c j e", u=2, e=2),
             )
+        nc.vector.quantize_mx(
+            out=w1_words[:].bitcast(FP8X4), scales=w1_scales[:], in_=w1_bf[:].rearrange("p t c j -> p (t c j)")
+        )
 
         def product(out, t, w_words, w_scales, words, scales):
             nc.tensor.matmul_mx(
@@ -119,106 +109,126 @@ def tile_picked_posadd_none_po_kernel(
                 stop=True,
             )
 
-        first = []
-
-        def first_product(c):
-            first.append(psum.tile([P, PACK, CH], F32, name=f"first{c}", tag=f"first{c % 2}"))
-            for t in range(PACK):
-                product(first[c][:, t, :], t, w1_words, w1_scales, xw_picked[:, chunk(c)], xs_picked[:, chunk(c)])
-
-        w2_bf = keep.tile([P, PACK, P, PACK], BF16, name="w2_bf", align_bytes=64)
-        w2_words = keep.tile([P, H], U32, name="w2_words", align_bytes=64)
-        w2_scales = keep.tile([P, H], U8, name="w2_scales", align_bytes=64)
-        deal(nc.scalar.copy, w2_bf, w2_raw[0], 0, 0, WH, 0, 2)
+        first = {}
         for u in range(2):
-            deal(nc.scalar.copy, w2_bf, w2_raw[1], WH, 0, WH, u, u + 1)
+            for a in (1 - u, u):
+                first[u, a] = psum.tile([P, 2, HALF], F32, name=f"first{u}{a}", tag=f"first{u}{a}")
+                for e in range(2):
+                    product(
+                        first[u, a][:, e, :], 2 * u + e, w1_words, w1_scales, xw_picked[:, half(a)], xs_picked[:, half(a)]
+                    )
 
-        def quantize_w2(t):
-            cols = slice(t * P, (t + 1) * P)
-            nc.vector.quantize_mx(
-                out=w2_words[:, cols].bitcast(FP8X4),
-                scales=w2_scales[:, cols],
-                in_=w2_bf[:, t].rearrange("p m j -> p (m j)"),
+        pe_picked = keep.tile([P, PACK, S], F32, name="pe_picked")
+
+        def scalar_gather(out, t, tokens):
+            nc.scalar.activation(out, pe_all[t][:].indirect(entries(tokens)), COPY)
+
+        def vector_gather(out, t, tokens):
+            nc.vector.tensor_copy(out, pe_all[t][:].indirect(entries(tokens)))
+
+        scalar_gather(pe_picked[:, 0, :], 0, slice(0, S))
+        scalar_gather(pe_picked[:, 1, half(0)], 1, half(0))
+        vector_gather(pe_picked[:, 1, half(1)], 1, half(1))
+        scalar_gather(pe_picked[:, 2, : LAST * CH], 2, slice(0, LAST * CH))
+        for c in range(LAST):
+            scalar_gather(pe_picked[:, 3, chunk(c)], 3, chunk(c))
+
+        h_bf = [keep.tile([P, HALF, PACK], BF16, name=f"h_bf{a}", align_bytes=64) for a in range(2)]
+        h_scales = [keep.tile([P, n], U8, name=f"h_scales{i}", align_bytes=64) for i, n in enumerate((HALF, CH, CH))]
+
+        def add(u, a, within, looked_up):
+            nc.vector.tensor_tensor(
+                woven(h_bf[a][:, within, pair(u)]), planar(first[u, a][:, :, within]), planar(looked_up), ADD
             )
-
-        h_front = keep.tile([P, HALF, PACK], BF16, name="h_front", align_bytes=64)
-        h_bf = [h_front[:, :CH], h_front[:, CH:], w2_bf[:, 0], w2_bf[:, 2]]
-        widths = (HALF, CH, CH)
-        tags = ("h_words0", "w2_raw1", "h_words2")
-        h_words = [
-            keep.tile([P, n], U32, name=f"h_words{i}", tag=tags[i], align_bytes=64) for i, n in enumerate(widths)
-        ]
-        h_scales = [keep.tile([P, n], U8, name=f"h_scales{i}", align_bytes=64) for i, n in enumerate(widths)]
-
-        def add(c):
-            nc.vector.tensor_tensor(woven(h_bf[c]), planar(first[c][:]), planar(pe_picked[:, :, chunk(c)]), ADD)
 
         def quantize_h(i, values):
             nc.vector.quantize_mx(
                 out=h_words[i][:].bitcast(FP8X4), scales=h_scales[i][:], in_=values.rearrange("p n t -> p (n t)")
             )
 
-        first_product(0)
-        first_product(1)
-        add(0)
-        first_product(2)
-        add(1)
-        first_product(3)
-        for c in range(2):
-            nc.vector.quantize_mx(
-                out=h_words[0][:, chunk(c)].bitcast(FP8X4),
-                scales=h_scales[0][:, chunk(c)],
-                in_=h_bf[c].rearrange("p n t -> p (n t)"),
+        w2_bf = [keep.tile([P, 2, P, PACK], BF16, name=f"w2_bf{u}", tag=f"w2_bf{u}", align_bytes=64) for u in range(2)]
+        h_words = [keep.tile([P, HALF], U32, name="h_words0", align_bytes=64)]
+        w2_words = keep.tile([P, H], U32, name="w2_words", align_bytes=64)
+        w2_scales = keep.tile([P, H], U8, name="w2_scales", align_bytes=64)
+
+        def round_w2(engine_copy, a, u, c0, c1):
+            engine_copy(
+                out=w2_bf[u][:, :, a * WH + c0 : a * WH + c1, :].rearrange("p e c j -> p c j e"),
+                in_=w2_raw[a][:].rearrange("p j (c u e) -> p u c j e", u=2, e=2)[:, u, c0:c1],
             )
-        quantize_w2(0)
-        quantize_w2(1)
-        add(2)
-        quantize_w2(2)
-        quantize_w2(3)
-        quantize_h(1, h_bf[2])
-        add(3)
-        quantize_h(2, h_bf[3])
+
+        for a in (1, 0):
+            add(0, a, slice(0, HALF), pe_picked[:, pair(0), half(a)])
+        for c in range(LAST):
+            add(1, c // 2, chunk(c % 2), pe_picked[:, pair(1), chunk(c)])
+        for u in range(2):
+            round_w2(nc.scalar.copy, 0, u, 0, WH)
+        quantize_h(0, h_bf[0][:])
+        for u in range(2):
+            round_w2(nc.vector.tensor_copy, 1, u, 0, W2_VECTOR[u])
+            round_w2(nc.scalar.copy, 1, u, W2_VECTOR[u], WH)
+        for t in range(PACK):
+            nc.vector.quantize_mx(
+                out=w2_words[:, t * P : (t + 1) * P].bitcast(FP8X4),
+                scales=w2_scales[:, t * P : (t + 1) * P],
+                in_=w2_bf[t // 2][:, t % 2].rearrange("p c j -> p (c j)"),
+            )
+
+        pe_last = w2_raw[1][:, 0, :].rearrange("p (e n) -> p e n", e=2)
+        scalar_gather(pe_last[:, 0, :], 2, chunk(LAST))
+        vector_gather(pe_last[:, 1, :], 3, chunk(LAST))
+        h_words.append(keep.tile([P, CH], U32, name="h_words1", tag="w2_bf1", align_bytes=64))
+        quantize_h(1, h_bf[1][:, chunk(0)])
+        add(1, 1, chunk(1), pe_last)
+        h_words.append(keep.tile([P, CH], U32, name="h_words2", align_bytes=64))
+        quantize_h(2, h_bf[1][:, chunk(1)])
 
         out_rows = out_0.rearrange("(p t) n -> p t n", t=PACK)
         out_words = out_1[0].rearrange("p n t -> p (n t)").bitcast(I32)
         y_front = keep.tile([P, PACK, HALF], F32, name="y_front")
-        for u in range(2):
-            bank = psum.tile([P, 2, HALF], F32, name=f"front{u}")
+        for t in range(2):
+            bank = psum.tile([P, HALF], F32, name=f"front{t}", tag=f"first0{t}")
+            product(bank[:], t, w2_words, w2_scales, h_words[0][:], h_scales[0][:])
+            nc.scalar.copy(out=y_front[:, t, :], in_=bank[:])
+        nc.sync.dma_start(out_rows[:, pair(0), half(0)], y_front[:, pair(0), :])
+        for c in range(2):
+            bank = psum.tile([P, 2, CH], F32, name=f"middle{c}")
             for e in range(2):
-                product(bank[:, e, :], 2 * u + e, w2_words, w2_scales, h_words[0][:], h_scales[0][:])
-            nc.scalar.copy(out=y_front[:, 2 * u : 2 * u + 2, :], in_=bank[:])
-            nc.sync.dma_start(out_rows[:, 2 * u : 2 * u + 2, half(0)], y_front[:, 2 * u : 2 * u + 2, :])
+                product(bank[:, e, :], 2 + e, w2_words, w2_scales, h_words[0][:, chunk(c)], h_scales[0][:, chunk(c)])
+            nc.scalar.copy(out=y_front[:, pair(1), chunk(c)], in_=bank[:])
+        nc.sync.dma_start(out_rows[:, pair(1), half(0)], y_front[:, pair(1), :])
         back = []
         y_back = []
-        for c in range(2, NCH):
-            bank = psum.tile([P, PACK, CH], F32, name=f"back{c}")
-            back.append(bank)
+        for c in range(2):
+            back.append(psum.tile([P, PACK, CH], F32, name=f"back{c}"))
             for t in range(PACK):
-                product(bank[:, t, :], t, w2_words, w2_scales, h_words[c - 1][:], h_scales[c - 1][:])
+                product(back[c][:, t, :], t, w2_words, w2_scales, h_words[1 + c][:], h_scales[1 + c][:])
             y_back.append(keep.tile([P, PACK, CH], F32, name=f"y_back{c}"))
-            nc.scalar.copy(out=y_back[-1][:], in_=bank[:])
-            nc.sync.dma_start(out_rows[:, :, chunk(c)], y_back[-1][:])
+            nc.scalar.copy(out=y_back[c][:], in_=back[c][:])
+            nc.sync.dma_start(out_rows[:, :, chunk(2 + c)], y_back[c][:])
 
-        y_bf = [keep.tile([P, n, PACK], BF16, name=f"y_bf{i}", align_bytes=64) for i, n in enumerate(widths)]
+        y_bf = [keep.tile([P, CH, PACK], BF16, name=f"y_bf{c}", align_bytes=64) for c in range(NCH)]
         y_words = keep.tile([P, S], U32, name="y_words", align_bytes=64)
         y_scales = keep.tile([P, S], U8, name="y_scales", align_bytes=64)
 
-        def quantize_y(i, tokens):
+        def quantize_y(c):
             nc.vector.quantize_mx(
-                out=y_words[:, tokens].bitcast(FP8X4),
-                scales=y_scales[:, tokens],
-                in_=y_bf[i][:].rearrange("p n t -> p (n t)"),
+                out=y_words[:, chunk(c)].bitcast(FP8X4),
+                scales=y_scales[:, chunk(c)],
+                in_=y_bf[c][:].rearrange("p n t -> p (n t)"),
             )
 
-        nc.scalar.copy(out=woven(y_bf[2][:]), in_=planar(back[1][:]))
-        nc.vector.tensor_copy(out=woven(y_bf[0][:]), in_=planar(y_front[:]))
-        nc.vector.tensor_copy(out=woven(y_bf[1][:]), in_=planar(y_back[0][:]))
-        quantize_y(0, half(0))
-        quantize_y(1, chunk(2))
-        nc.sync.dma_start(out_words[:, : 3 * CH], y_words[:, : 3 * CH].bitcast(I32))
-        quantize_y(2, chunk(3))
-        nc.sync.dma_start(out_words[:, chunk(3)], y_words[:, chunk(3)].bitcast(I32))
+        for c in range(2):
+            nc.vector.tensor_copy(out=woven(y_bf[c][:]), in_=planar(y_front[:, :, chunk(c)]))
+        quantize_y(0)
+        nc.vector.tensor_copy(out=woven(y_bf[2][:]), in_=planar(y_back[0][:]))
+        quantize_y(1)
+        nc.sync.dma_start(out_words[:, half(0)], y_words[:, half(0)].bitcast(I32))
+        nc.scalar.copy(out=woven(y_bf[LAST][:]), in_=planar(back[1][:]))
+        quantize_y(2)
+        quantize_y(LAST)
+        nc.sync.dma_start(out_words[:, half(1)], y_words[:, half(1)].bitcast(I32))
         for q in range(QUADRANTS):
-            nc.sync.dma_start(
+            (nc.sync, nc.scalar)[q % 2].dma_start(
                 out_2[0, 4 * q : 4 * q + 4, :].bitcast(I32), y_scales[32 * q : 32 * q + 4, :].bitcast(I32)
             )

@@ -23,6 +23,7 @@ CH = 128
 NCH = S // CH
 LAST = NCH - 1
 HALF = S // 2
+DMA_ALIGN = 256
 WH = P // 2
 W2_VECTOR = (40, 24)
 
@@ -56,9 +57,9 @@ def tile_picked_posadd_none_po_kernel(
         psum = ctx.enter_context(tc.psum_pool(name="psum", bufs=1))
 
         offsets = keep.tile([P, S // LIST_ROWS], U16, name="offsets")
-        xs_all = keep.tile([P, T], U8, name="xs_all", align_bytes=64)
+        xs_all = keep.tile([P, T], U8, name="xs_all", align_bytes=DMA_ALIGN)
         nc.vector.memset(xs_all[:].bitcast(I32), 0)
-        xw_all = keep.tile([P, T], U32, name="xw_all", align_bytes=64)
+        xw_all = keep.tile([P, T], U32, name="xw_all", align_bytes=DMA_ALIGN)
         nc.sync.dma_start(xw_all[:].bitcast(I32), x_words[0].rearrange("p n t -> p (n t)").bitcast(I32))
         nc.sync.dma_start(offsets[:], offs)
         for q in range(QUADRANTS):
@@ -68,9 +69,9 @@ def tile_picked_posadd_none_po_kernel(
         w1_rows = w1.rearrange("(p j) c -> p j c", j=PACK)
         w2_rows = w2.rearrange("(p j) c -> p j c", j=PACK)
         pe_rows = pe.rearrange("(p t) c -> p t c", t=PACK)
-        w1_raw = [keep.tile([P, PACK, H // 2], F32, name=f"w1_raw{a}") for a in range(2)]
-        w2_raw = [keep.tile([P, PACK, H // 2], F32, name=f"w2_raw{a}") for a in range(2)]
-        pe_all = [keep.tile([P, T], F32, name=f"pe_all{t}") for t in range(PACK)]
+        w1_raw = [keep.tile([P, PACK, H // 2], F32, name=f"w1_raw{a}", align_bytes=DMA_ALIGN) for a in range(2)]
+        w2_raw = [keep.tile([P, PACK, H // 2], F32, name=f"w2_raw{a}", align_bytes=DMA_ALIGN) for a in range(2)]
+        pe_all = [keep.tile([P, T], F32, name=f"pe_all{t}", align_bytes=DMA_ALIGN) for t in range(PACK)]
         for a in range(2):
             nc.sync.dma_start(w1_raw[a][:], w1_rows[:, :, half(a)])
         for t in range(PACK):
@@ -185,7 +186,7 @@ def tile_picked_posadd_none_po_kernel(
 
         out_rows = out_0.rearrange("(p t) n -> p t n", t=PACK)
         out_words = out_1[0].rearrange("p n t -> p (n t)").bitcast(I32)
-        y_front = keep.tile([P, PACK, HALF], F32, name="y_front")
+        y_front = keep.tile([P, PACK, HALF], F32, name="y_front", align_bytes=DMA_ALIGN)
         for t in range(2):
             bank = psum.tile([P, HALF], F32, name=f"front{t}", tag=f"first0{t}")
             product(bank[:], t, w2_words, w2_scales, h_words[0][:], h_scales[0][:])
@@ -203,13 +204,13 @@ def tile_picked_posadd_none_po_kernel(
             back.append(psum.tile([P, PACK, CH], F32, name=f"back{c}"))
             for t in range(PACK):
                 product(back[c][:, t, :], t, w2_words, w2_scales, h_words[1 + c][:], h_scales[1 + c][:])
-            y_back.append(keep.tile([P, PACK, CH], F32, name=f"y_back{c}"))
+            y_back.append(keep.tile([P, PACK, CH], F32, name=f"y_back{c}", align_bytes=DMA_ALIGN))
             nc.scalar.copy(out=y_back[c][:], in_=back[c][:])
             nc.sync.dma_start(out_rows[:, :, chunk(2 + c)], y_back[c][:])
 
         y_bf = [keep.tile([P, CH, PACK], BF16, name=f"y_bf{c}", align_bytes=64) for c in range(NCH)]
-        y_words = keep.tile([P, S], U32, name="y_words", align_bytes=64)
-        y_scales = keep.tile([P, S], U8, name="y_scales", align_bytes=64)
+        y_words = keep.tile([P, S], U32, name="y_words", align_bytes=DMA_ALIGN)
+        y_scales = keep.tile([P, S], U8, name="y_scales", align_bytes=DMA_ALIGN)
 
         def quantize_y(c):
             nc.vector.quantize_mx(

@@ -23,7 +23,7 @@ CH = 128
 NCH = S // CH
 LAST = NCH - 1
 HALF = S // 2
-DMA_ALIGN = 256
+ALIGN = 256
 WH = P // 2
 W2_VECTOR = (40, 24)
 
@@ -57,9 +57,9 @@ def tile_picked_posadd_none_po_kernel(
         psum = ctx.enter_context(tc.psum_pool(name="psum", bufs=1))
 
         offsets = keep.tile([P, S // LIST_ROWS], U16, name="offsets")
-        xs_all = keep.tile([P, T], U8, name="xs_all", align_bytes=DMA_ALIGN)
+        xs_all = keep.tile([P, T], U8, name="xs_all", align_bytes=ALIGN)
         nc.vector.memset(xs_all[:].bitcast(I32), 0)
-        xw_all = keep.tile([P, T], U32, name="xw_all", align_bytes=DMA_ALIGN)
+        xw_all = keep.tile([P, T], U32, name="xw_all", align_bytes=ALIGN)
         nc.sync.dma_start(xw_all[:].bitcast(I32), x_words[0].rearrange("p n t -> p (n t)").bitcast(I32))
         nc.sync.dma_start(offsets[:], offs)
         for q in range(QUADRANTS):
@@ -69,9 +69,9 @@ def tile_picked_posadd_none_po_kernel(
         w1_rows = w1.rearrange("(p j) c -> p j c", j=PACK)
         w2_rows = w2.rearrange("(p j) c -> p j c", j=PACK)
         pe_rows = pe.rearrange("(p t) c -> p t c", t=PACK)
-        w1_raw = [keep.tile([P, PACK, H // 2], F32, name=f"w1_raw{a}", align_bytes=DMA_ALIGN) for a in range(2)]
-        w2_raw = [keep.tile([P, PACK, H // 2], F32, name=f"w2_raw{a}", align_bytes=DMA_ALIGN) for a in range(2)]
-        pe_all = [keep.tile([P, T], F32, name=f"pe_all{t}", align_bytes=DMA_ALIGN) for t in range(PACK)]
+        w1_raw = [keep.tile([P, PACK, H // 2], F32, name=f"w1_raw{a}", align_bytes=ALIGN) for a in range(2)]
+        w2_raw = [keep.tile([P, PACK, H // 2], F32, name=f"w2_raw{a}", align_bytes=ALIGN) for a in range(2)]
+        pe_all = [keep.tile([P, T], F32, name=f"pe_all{t}", align_bytes=ALIGN) for t in range(PACK)]
         for a in range(2):
             nc.sync.dma_start(w1_raw[a][:], w1_rows[:, :, half(a)])
         for t in range(PACK):
@@ -82,14 +82,14 @@ def tile_picked_posadd_none_po_kernel(
         def entries(tokens):
             return offsets[:, tokens.start // LIST_ROWS : tokens.stop // LIST_ROWS]
 
-        xw_picked = keep.tile([P, S], U32, name="xw_picked", align_bytes=64)
+        xw_picked = keep.tile([P, S], U32, name="xw_picked", align_bytes=ALIGN)
         nc.vector.tensor_copy(xw_picked[:], xw_all[:].indirect(offsets[:]))
-        xs_picked = keep.tile([P, S], U8, name="xs_picked", align_bytes=64)
+        xs_picked = keep.tile([P, S], U8, name="xs_picked", align_bytes=ALIGN)
         nc.vector.tensor_copy(xs_picked[:], xs_all[:].indirect(offsets[:]))
 
-        w1_bf = keep.tile([P, PACK, P, PACK], BF16, name="w1_bf", align_bytes=64)
-        w1_words = keep.tile([P, H], U32, name="w1_words", align_bytes=64)
-        w1_scales = keep.tile([P, H], U8, name="w1_scales", align_bytes=64)
+        w1_bf = keep.tile([P, PACK, P, PACK], BF16, name="w1_bf", align_bytes=ALIGN)
+        w1_words = keep.tile([P, H], U32, name="w1_words", align_bytes=ALIGN)
+        w1_scales = keep.tile([P, H], U8, name="w1_scales", align_bytes=ALIGN)
         for a, engine_copy in enumerate((nc.scalar.copy, nc.vector.tensor_copy)):
             engine_copy(
                 out=w1_bf[:, :, a * WH : (a + 1) * WH, :].rearrange("p (u e) c j -> p u c j e", e=2),
@@ -119,7 +119,7 @@ def tile_picked_posadd_none_po_kernel(
                         first[u, a][:, e, :], 2 * u + e, w1_words, w1_scales, xw_picked[:, half(a)], xs_picked[:, half(a)]
                     )
 
-        pe_picked = keep.tile([P, PACK, S], F32, name="pe_picked")
+        pe_picked = keep.tile([P, PACK, S], F32, name="pe_picked", align_bytes=ALIGN)
 
         def scalar_gather(out, t, tokens):
             nc.scalar.activation(out, pe_all[t][:].indirect(entries(tokens)), COPY)
@@ -134,8 +134,8 @@ def tile_picked_posadd_none_po_kernel(
         for c in range(LAST):
             scalar_gather(pe_picked[:, 3, chunk(c)], 3, chunk(c))
 
-        h_bf = [keep.tile([P, HALF, PACK], BF16, name=f"h_bf{a}", align_bytes=64) for a in range(2)]
-        h_scales = [keep.tile([P, n], U8, name=f"h_scales{i}", align_bytes=64) for i, n in enumerate((HALF, CH, CH))]
+        h_bf = [keep.tile([P, HALF, PACK], BF16, name=f"h_bf{a}", align_bytes=ALIGN) for a in range(2)]
+        h_scales = [keep.tile([P, n], U8, name=f"h_scales{i}", align_bytes=ALIGN) for i, n in enumerate((HALF, CH, CH))]
 
         def add(u, a, within, looked_up):
             nc.vector.tensor_tensor(
@@ -147,10 +147,10 @@ def tile_picked_posadd_none_po_kernel(
                 out=h_words[i][:].bitcast(FP8X4), scales=h_scales[i][:], in_=values.rearrange("p n t -> p (n t)")
             )
 
-        w2_bf = [keep.tile([P, 2, P, PACK], BF16, name=f"w2_bf{u}", tag=f"w2_bf{u}", align_bytes=64) for u in range(2)]
-        h_words = [keep.tile([P, HALF], U32, name="h_words0", align_bytes=64)]
-        w2_words = keep.tile([P, H], U32, name="w2_words", align_bytes=64)
-        w2_scales = keep.tile([P, H], U8, name="w2_scales", align_bytes=64)
+        w2_bf = [keep.tile([P, 2, P, PACK], BF16, name=f"w2_bf{u}", tag=f"w2_bf{u}", align_bytes=ALIGN) for u in range(2)]
+        h_words = [keep.tile([P, HALF], U32, name="h_words0", align_bytes=ALIGN)]
+        w2_words = keep.tile([P, H], U32, name="w2_words", align_bytes=ALIGN)
+        w2_scales = keep.tile([P, H], U8, name="w2_scales", align_bytes=ALIGN)
 
         def round_w2(engine_copy, a, u, c0, c1):
             engine_copy(
@@ -178,15 +178,26 @@ def tile_picked_posadd_none_po_kernel(
         pe_last = w2_raw[1][:, 0, :].rearrange("p (e n) -> p e n", e=2)
         scalar_gather(pe_last[:, 0, :], 2, chunk(LAST))
         vector_gather(pe_last[:, 1, :], 3, chunk(LAST))
-        h_words.append(keep.tile([P, CH], U32, name="h_words1", tag="w2_bf1", align_bytes=64))
+        h_words.append(keep.tile([P, CH], U32, name="h_words1", tag="w2_bf1", align_bytes=ALIGN))
         quantize_h(1, h_bf[1][:, chunk(0)])
         add(1, 1, chunk(1), pe_last)
-        h_words.append(keep.tile([P, CH], U32, name="h_words2", align_bytes=64))
+        h_words.append(keep.tile([P, CH], U32, name="h_words2", align_bytes=ALIGN))
         quantize_h(2, h_bf[1][:, chunk(1)])
+
+        y_bf = [keep.tile([P, CH, PACK], BF16, name=f"y_bf{c}", align_bytes=ALIGN) for c in range(NCH)]
+        y_words = keep.tile([P, S], U32, name="y_words", align_bytes=ALIGN)
+        y_scales = keep.tile([P, S], U8, name="y_scales", align_bytes=ALIGN)
+
+        def quantize_y(c):
+            nc.vector.quantize_mx(
+                out=y_words[:, chunk(c)].bitcast(FP8X4),
+                scales=y_scales[:, chunk(c)],
+                in_=y_bf[c][:].rearrange("p n t -> p (n t)"),
+            )
 
         out_rows = out_0.rearrange("(p t) n -> p t n", t=PACK)
         out_words = out_1[0].rearrange("p n t -> p (n t)").bitcast(I32)
-        y_front = keep.tile([P, PACK, HALF], F32, name="y_front", align_bytes=DMA_ALIGN)
+        y_front = keep.tile([P, PACK, HALF], F32, name="y_front", align_bytes=ALIGN)
         for t in range(2):
             bank = psum.tile([P, HALF], F32, name=f"front{t}", tag=f"first0{t}")
             product(bank[:], t, w2_words, w2_scales, h_words[0][:], h_scales[0][:])
@@ -198,34 +209,25 @@ def tile_picked_posadd_none_po_kernel(
                 product(bank[:, e, :], 2 + e, w2_words, w2_scales, h_words[0][:, chunk(c)], h_scales[0][:, chunk(c)])
             nc.scalar.copy(out=y_front[:, pair(1), chunk(c)], in_=bank[:])
         nc.sync.dma_start(out_rows[:, pair(1), half(0)], y_front[:, pair(1), :])
-        back = []
-        y_back = []
-        for c in range(2):
-            back.append(psum.tile([P, PACK, CH], F32, name=f"back{c}"))
-            for t in range(PACK):
-                product(back[c][:, t, :], t, w2_words, w2_scales, h_words[1 + c][:], h_scales[1 + c][:])
-            y_back.append(keep.tile([P, PACK, CH], F32, name=f"y_back{c}", align_bytes=DMA_ALIGN))
-            nc.scalar.copy(out=y_back[c][:], in_=back[c][:])
-            nc.sync.dma_start(out_rows[:, :, chunk(2 + c)], y_back[c][:])
-
-        y_bf = [keep.tile([P, CH, PACK], BF16, name=f"y_bf{c}", align_bytes=64) for c in range(NCH)]
-        y_words = keep.tile([P, S], U32, name="y_words", align_bytes=DMA_ALIGN)
-        y_scales = keep.tile([P, S], U8, name="y_scales", align_bytes=DMA_ALIGN)
-
-        def quantize_y(c):
-            nc.vector.quantize_mx(
-                out=y_words[:, chunk(c)].bitcast(FP8X4),
-                scales=y_scales[:, chunk(c)],
-                in_=y_bf[c][:].rearrange("p n t -> p (n t)"),
-            )
-
+        y_back = [keep.tile([P, PACK, CH], F32, name=f"y_back{c}", align_bytes=ALIGN) for c in range(2)]
+        third = psum.tile([P, PACK, CH], F32, name="third")
+        for t in range(PACK):
+            product(third[:, t, :], t, w2_words, w2_scales, h_words[1][:], h_scales[1][:])
+        nc.scalar.copy(out=y_back[0][:], in_=third[:])
+        nc.sync.dma_start(out_rows[:, :, chunk(2)], y_back[0][:])
         for c in range(2):
             nc.vector.tensor_copy(out=woven(y_bf[c][:]), in_=planar(y_front[:, :, chunk(c)]))
-        quantize_y(0)
-        nc.vector.tensor_copy(out=woven(y_bf[2][:]), in_=planar(y_back[0][:]))
-        quantize_y(1)
+        for c in range(2):
+            quantize_y(c)
         nc.sync.dma_start(out_words[:, half(0)], y_words[:, half(0)].bitcast(I32))
-        nc.scalar.copy(out=woven(y_bf[LAST][:]), in_=planar(back[1][:]))
+        for u, (tag, engine_copy) in enumerate((("last", nc.scalar.copy), ("first11", nc.vector.tensor_copy))):
+            bank = psum.tile([P, 2, CH], F32, name=f"last{u}", tag=tag)
+            for e in range(2):
+                product(bank[:, e, :], 2 * u + e, w2_words, w2_scales, h_words[2][:], h_scales[2][:])
+            engine_copy(out=y_back[1][:, pair(u), :], in_=bank[:])
+        nc.sync.dma_start(out_rows[:, :, chunk(LAST)], y_back[1][:])
+        nc.scalar.copy(out=woven(y_bf[2][:]), in_=planar(third[:]))
+        nc.vector.tensor_copy(out=woven(y_bf[LAST][:]), in_=planar(y_back[1][:]))
         quantize_y(2)
         quantize_y(LAST)
         nc.sync.dma_start(out_words[:, half(1)], y_words[:, half(1)].bitcast(I32))

from contextlib import ExitStack

import concourse.mybir as mybir

K, T, S, H = 512, 1024, 512, 512
FLOPS = 2 * K * H * S + 2 * H * H * S

F32 = mybir.dt.float32
BF16 = mybir.dt.bfloat16
I32 = mybir.dt.int32
U32 = mybir.dt.uint32
U16 = mybir.dt.uint16
U8 = mybir.dt.uint8
FP8X4 = mybir.dt.float8_e4m3fn_x4
ADD = mybir.AluOpType.add
COPY = mybir.ActivationFunctionType.Copy

P = 128
PACK = 4
QUADRANTS = 4
LIST_ROWS = 16
CH = 128
NCH = S // CH
LAST = NCH - 1
HALF = S // 2
ALIGN = 256
WH = P // 2
W2_VECTOR = (40, 24)


def woven(tile):
    return tile.rearrange("p (c i) t -> p c t i", i=2)


def planar(tile):
    return tile.rearrange("p t (c i) -> p c t i", i=2)


def chunk(c):
    return slice(c * CH, (c + 1) * CH)


def half(a):
    return slice(a * HALF, (a + 1) * HALF)


def pair(u):
    return slice(2 * u, 2 * u + 2)


def tile_picked_posadd_none_po_kernel(
    tc, x_words, x_scales, w1, w2, pe, offs, out_0, out_1, out_2
):
    nc = tc.nc
    with ExitStack() as ctx:
        keep = ctx.enter_context(tc.tile_pool(name="keep", bufs=1))
        psum = ctx.enter_context(tc.psum_pool(name="psum", bufs=1))

        offsets = keep.tile([P, S // LIST_ROWS], U16, name="offsets")
        xs_all = keep.tile([P, T], U8, name="xs_all", align_bytes=ALIGN)
        nc.vector.memset(xs_all[:].bitcast(I32), 0)
        xw_all = keep.tile([P, T], U32, name="xw_all", align_bytes=ALIGN)
        nc.sync.dma_start(xw_all[:].bitcast(I32), x_words[0].rearrange("p n t -> p (n t)").bitcast(I32))
        nc.sync.dma_start(offsets[:], offs)
        for q in range(QUADRANTS):
            nc.sync.dma_start(
                xs_all[32 * q : 32 * q + 4, :].bitcast(I32), x_scales[0, 4 * q : 4 * q + 4, :].bitcast(I32)
            )
        w1_rows = w1.rearrange("(p j) c -> p j c", j=PACK)
        w2_rows = w2.rearrange("(p j) c -> p j c", j=PACK)
        pe_rows = pe.rearrange("(p t) c -> p t c", t=PACK)
        w1_raw = [keep.tile([P, PACK, H // 2], F32, name=f"w1_raw{a}", align_bytes=ALIGN) for a in range(2)]
        w2_raw = [keep.tile([P, PACK, H // 2], F32, name=f"w2_raw{a}", align_bytes=ALIGN) for a in range(2)]
        pe_all = [keep.tile([P, T], F32, name=f"pe_all{t}", align_bytes=ALIGN) for t in range(PACK)]
        for a in range(2):
            nc.sync.dma_start(w1_raw[a][:], w1_rows[:, :, half(a)])
        for t in range(PACK):
            nc.sync.dma_start(pe_all[t][:], pe_rows[:, t, :])
        for a in range(2):
            nc.sync.dma_start(w2_raw[a][:], w2_rows[:, :, half(a)])

        def entries(tokens):
            return offsets[:, tokens.start // LIST_ROWS : tokens.stop // LIST_ROWS]

        xw_picked = keep.tile([P, S], U32, name="xw_picked", align_bytes=ALIGN)
        nc.vector.tensor_copy(xw_picked[:], xw_all[:].indirect(offsets[:]))
        xs_picked = keep.tile([P, S], U8, name="xs_picked", align_bytes=ALIGN)
        nc.vector.tensor_copy(xs_picked[:], xs_all[:].indirect(offsets[:]))

        w1_bf = keep.tile([P, PACK, P, PACK], BF16, name="w1_bf", align_bytes=ALIGN)
        w1_words = keep.tile([P, H], U32, name="w1_words", align_bytes=ALIGN)
        w1_scales = keep.tile([P, H], U8, name="w1_scales", align_bytes=ALIGN)
        for a, engine_copy in enumerate((nc.scalar.copy, nc.vector.tensor_copy)):
            engine_copy(
                out=w1_bf[:, :, a * WH : (a + 1) * WH, :].rearrange("p (u e) c j -> p u c j e", e=2),
                in_=w1_raw[a][:].rearrange("p j (c u e) -> p u c j e", u=2, e=2),
            )
        nc.vector.quantize_mx(
            out=w1_words[:].bitcast(FP8X4), scales=w1_scales[:], in_=w1_bf[:].rearrange("p t c j -> p (t c j)")
        )

        def product(out, t, w_words, w_scales, words, scales):
            nc.tensor.matmul_mx(
                out=out,
                lhsT=w_words[:, t * P : (t + 1) * P].bitcast(FP8X4),
                lhsT_scale=w_scales[:, t * P : (t + 1) * P],
                rhs=words.bitcast(FP8X4),
                rhs_scale=scales,
                start=True,
                stop=True,
            )

        first = {}
        for u in range(2):
            for a in (1 - u, u):
                first[u, a] = psum.tile([P, 2, HALF], F32, name=f"first{u}{a}", tag=f"first{u}{a}")
                for e in range(2):
                    product(
                        first[u, a][:, e, :], 2 * u + e, w1_words, w1_scales, xw_picked[:, half(a)], xs_picked[:, half(a)]
                    )

        pe_picked = keep.tile([P, PACK, S], F32, name="pe_picked", align_bytes=ALIGN)

        def scalar_gather(out, t, tokens):
            nc.scalar.activation(out, pe_all[t][:].indirect(entries(tokens)), COPY)

        def vector_gather(out, t, tokens):
            nc.vector.tensor_copy(out, pe_all[t][:].indirect(entries(tokens)))

        scalar_gather(pe_picked[:, 0, :], 0, slice(0, S))
        scalar_gather(pe_picked[:, 1, half(0)], 1, half(0))
        vector_gather(pe_picked[:, 1, half(1)], 1, half(1))
        scalar_gather(pe_picked[:, 2, : LAST * CH], 2, slice(0, LAST * CH))
        for c in range(LAST):
            scalar_gather(pe_picked[:, 3, chunk(c)], 3, chunk(c))

        h_bf = [keep.tile([P, HALF, PACK], BF16, name=f"h_bf{a}", align_bytes=ALIGN) for a in range(2)]
        h_scales = [keep.tile([P, n], U8, name=f"h_scales{i}", align_bytes=ALIGN) for i, n in enumerate((HALF, CH, CH))]

        def add(u, a, within, looked_up):
            nc.vector.tensor_tensor(
                woven(h_bf[a][:, within, pair(u)]), planar(first[u, a][:, :, within]), planar(looked_up), ADD
            )

        def quantize_h(i, values):
            nc.vector.quantize_mx(
                out=h_words[i][:].bitcast(FP8X4), scales=h_scales[i][:], in_=values.rearrange("p n t -> p (n t)")
            )

        w2_bf = [keep.tile([P, 2, P, PACK], BF16, name=f"w2_bf{u}", tag=f"w2_bf{u}", align_bytes=ALIGN) for u in range(2)]
        h_words = [keep.tile([P, HALF], U32, name="h_words0", align_bytes=ALIGN)]
        w2_words = keep.tile([P, H], U32, name="w2_words", align_bytes=ALIGN)
        w2_scales = keep.tile([P, H], U8, name="w2_scales", align_bytes=ALIGN)

        def round_w2(engine_copy, a, u, c0, c1):
            engine_copy(
                out=w2_bf[u][:, :, a * WH + c0 : a * WH + c1, :].rearrange("p e c j -> p c j e"),
                in_=w2_raw[a][:].rearrange("p j (c u e) -> p u c j e", u=2, e=2)[:, u, c0:c1],
            )

        for a in (1, 0):
            add(0, a, slice(0, HALF), pe_picked[:, pair(0), half(a)])
        for c in range(LAST):
            add(1, c // 2, chunk(c % 2), pe_picked[:, pair(1), chunk(c)])
        for u in range(2):
            round_w2(nc.scalar.copy, 0, u, 0, WH)
        quantize_h(0, h_bf[0][:])
        for u in range(2):
            round_w2(nc.vector.tensor_copy, 1, u, 0, W2_VECTOR[u])
            round_w2(nc.scalar.copy, 1, u, W2_VECTOR[u], WH)
        for t in range(PACK):
            nc.vector.quantize_mx(
                out=w2_words[:, t * P : (t + 1) * P].bitcast(FP8X4),
                scales=w2_scales[:, t * P : (t + 1) * P],
                in_=w2_bf[t // 2][:, t % 2].rearrange("p c j -> p (c j)"),
            )

        pe_last = w2_raw[1][:, 0, :].rearrange("p (e n) -> p e n", e=2)
        scalar_gather(pe_last[:, 0, :], 2, chunk(LAST))
        vector_gather(pe_last[:, 1, :], 3, chunk(LAST))
        h_words.append(keep.tile([P, CH], U32, name="h_words1", tag="w2_bf1", align_bytes=ALIGN))
        quantize_h(1, h_bf[1][:, chunk(0)])
        add(1, 1, chunk(1), pe_last)
        h_words.append(keep.tile([P, CH], U32, name="h_words2", align_bytes=ALIGN))
        quantize_h(2, h_bf[1][:, chunk(1)])

        y_bf = [keep.tile([P, CH, PACK], BF16, name=f"y_bf{c}", align_bytes=ALIGN) for c in range(NCH)]
        y_words = keep.tile([P, S], U32, name="y_words", align_bytes=ALIGN)
        y_scales = keep.tile([P, S], U8, name="y_scales", align_bytes=ALIGN)

        def quantize_y(c):
            nc.vector.quantize_mx(
                out=y_words[:, chunk(c)].bitcast(FP8X4),
                scales=y_scales[:, chunk(c)],
                in_=y_bf[c][:].rearrange("p n t -> p (n t)"),
            )

        out_rows = out_0.rearrange("(p t) n -> p t n", t=PACK)
        out_words = out_1[0].rearrange("p n t -> p (n t)").bitcast(I32)
        y_front = keep.tile([P, PACK, HALF], F32, name="y_front", align_bytes=ALIGN)
        for t in range(2):
            bank = psum.tile([P, HALF], F32, name=f"front{t}", tag=f"first0{t}")
            product(bank[:], t, w2_words, w2_scales, h_words[0][:], h_scales[0][:])
            nc.scalar.copy(out=y_front[:, t, :], in_=bank[:])
        nc.sync.dma_start(out_rows[:, pair(0), half(0)], y_front[:, pair(0), :])
        for c in range(2):
            bank = psum.tile([P, 2, CH], F32, name=f"middle{c}")
            for e in range(2):
                product(bank[:, e, :], 2 + e, w2_words, w2_scales, h_words[0][:, chunk(c)], h_scales[0][:, chunk(c)])
            nc.scalar.copy(out=y_front[:, pair(1), chunk(c)], in_=bank[:])
        nc.sync.dma_start(out_rows[:, pair(1), half(0)], y_front[:, pair(1), :])
        y_back = [keep.tile([P, PACK, CH], F32, name=f"y_back{c}", align_bytes=ALIGN) for c in range(2)]
        third = psum.tile([P, PACK, CH], F32, name="third")
        for t in range(PACK):
            product(third[:, t, :], t, w2_words, w2_scales, h_words[1][:], h_scales[1][:])
        nc.scalar.copy(out=y_back[0][:], in_=third[:])
        nc.sync.dma_start(out_rows[:, :, chunk(2)], y_back[0][:])
        for c in range(2):
            nc.vector.tensor_copy(out=woven(y_bf[c][:]), in_=planar(y_front[:, :, chunk(c)]))
        for c in range(2):
            quantize_y(c)
        nc.sync.dma_start(out_words[:, half(0)], y_words[:, half(0)].bitcast(I32))
        for u, (tag, engine_copy) in enumerate((("last", nc.scalar.copy), ("first11", nc.vector.tensor_copy))):
            bank = psum.tile([P, 2, CH], F32, name=f"last{u}", tag=tag)
            for e in range(2):
                product(bank[:, e, :], 2 * u + e, w2_words, w2_scales, h_words[2][:], h_scales[2][:])
            engine_copy(out=y_back[1][:, pair(u), :], in_=bank[:])
        nc.sync.dma_start(out_rows[:, :, chunk(LAST)], y_back[1][:])
        nc.scalar.copy(out=woven(y_bf[2][:]), in_=planar(third[:]))
        nc.vector.tensor_copy(out=woven(y_bf[LAST][:]), in_=planar(y_back[1][:]))
        quantize_y(2)
        quantize_y(LAST)
        nc.sync.dma_start(out_words[:, half(1)], y_words[:, half(1)].bitcast(I32))
        for q in range(QUADRANTS):
            (nc.sync, nc.scalar)[q % 2].dma_start(
                out_2[0, 4 * q : 4 * q + 4, :].bitcast(I32), y_scales[32 * q : 32 * q + 4, :].bitcast(I32)
            )
